import numpy as np, ml_dtypes
CORES = [16,17,18,19,32,33,34,35]
N = 8
BF = ml_dtypes.bfloat16
def gentries(a):
    return np.ascontiguousarray(a.reshape(8, 16, -1).transpose(0, 2, 1)).reshape(8, -1)
def gtable(e):
    e = np.asarray(e); return np.ascontiguousarray(e.reshape(8, -1, 16).transpose(0, 2, 1)).reshape(128, -1).astype(np.int32)
W, UN, P, SH, MS = 8192, 192, 16, 4, (1, 2)
def parts(rng):
    e = (0.5 + 2.5 * rng.random((N, 8, 16, 1))).astype(np.float32)
    sh = np.minimum(np.floor(256 * rng.random((N, 8, 16, W), dtype=np.float32) ** e), 255)
    return sh, rng.integers(0, W, (N, 8, UN, P))
def pack(sh, un):
    return {"shelf": np.ascontiguousarray(sh.reshape(N, 128, W)).astype(np.float32).astype(BF), "units": np.stack([gtable(a.reshape(8, -1)) for a in un])}
def setup_inputs(rng):
    sh, un = parts(rng)
    return pack(sh, un)
def setup_inputs_ties(rng):
    sh, un = parts(rng)
    sh = (rng.random((N, 8, 16, W)) < 0.03) * rng.choice(np.array([1, 7, 255]), (1, 8, 1, 1))
    sh[:, rng.integers(0, 8)] = 9
    return pack(sh, un)
def setup_inputs_alike(rng):
    sh, un = parts(rng)
    un[:, 0] = un[0, 0].copy()
    un[:, 1] = rng.choice(np.array([0, 1, W - 1, W // 2]), (N, UN, P))
    un[:, 2] = un[:, 2, :1].copy()
    un[:, 3] = un[:, 3, :, :1].copy()
    un[:, 4] = 0
    un[:, 5, 1::2] = un[:, 5, ::2].copy()
    un[:, 6, :, P // 2:] = un[:1, 6, :1, P // 2:].copy()
    return pack(sh, un)
def setup_inputs_ends(rng):
    sh, un = parts(rng)
    sh[:, :7] = sh[:1, :7].copy(); x = rng.integers(1, W, (N, 7, UN)); un[:, :7] = 0
    for g, e in enumerate((0, P - 1, P // 2 - 1, P // 2, 1, P - 2, int(rng.integers(0, P)))): un[:, g, :, e] = x[:, g]
    return pack(sh, un)
def setup_inputs_rare(rng):
    sh, un = parts(rng)
    few = W // (8 * P) * np.array([1, 2, 3, 4, 2, 3])[:, None, None]
    hit = np.argsort(rng.random((N, 6, 1, W)), axis=-1) < few
    v = rng.integers(1, 256, (N, 6, 16, W)); v[:, 0] = 1; v[:, 1] = 255
    v = np.where(hit, v, 0); v[:, 4:] = 255 - v[:, 4:]
    sh[:, :6] = v
    sh[:, 6] = rng.choice(np.array([0, 1, 2, 253, 254, 255]), (N, 16, W))
    sh[:, 7] = np.clip(rng.integers(-64, 320, (N, 16, W)), 0, 255)
    sh = np.where((sh == 0) & (rng.random(sh.shape, dtype=np.float32) < 0.5), np.float32(-0.0), sh)
    return pack(sh, un)
def setup_inputs_spread(rng):
    sh, un = parts(rng)
    k = np.exp2(8 * rng.random((N, 8, 1, W))) * (rng.random((N, 8, 1, W)) > 0.0625)
    sh = np.minimum(np.floor(rng.random((N, 8, 16, W)) * k), 255)
    un = np.minimum((W * rng.random((N, 8, UN, P)) ** rng.choice(np.array([1, 2, 4, 8]), (N, 8, 1, 1))).astype(np.int64), W - 1)
    return pack(sh, un)
def check_inputs(d):
    bad = []; v = np.asarray(d["shelf"]).astype(np.float32)
    if not np.all((v >= 0) & (v <= 255) & (v == np.floor(v))): bad.append("values of shelf")
    if np.min(d["units"]) < 0 or np.max(d["units"]) > W - 1: bad.append("range of units")
    return bad
def reference(shelf, units):
    tab = np.ascontiguousarray(shelf.astype(np.float32).astype(np.int16).reshape(N, 8, 16, W).transpose(0, 1, 3, 2))
    un = np.stack([gentries(a) for a in units]).astype(np.int64).reshape(N, 8, UN, P)
    A = np.zeros((N, 8), np.int64); rank = np.arange(N); place = np.arange(P)
    n3, g3 = rank[:, None, None], np.arange(8)[None, :, None]
    def measure(x):
        z = (A[:, :, None, None] + np.add.accumulate(x, axis=3)) & 4095
        c = ((z * z >> SH) + x) & (W - 1)
        b = tab[n3[..., None], g3[..., None], c]
        return np.sum((np.max(b, axis=3) - np.min(b, axis=3)).astype(np.int64), axis=3)
    for m in MS:
        mate = rank ^ m; low = (rank < mate)[:, None, None]
        q = measure(un)
        order = np.argsort(np.where(low, -q, q), axis=2, kind="stable")
        own = un[n3, g3, order]; qo = q[n3, g3, order]; far = own[mate]; qf = qo[mate]
        s0 = np.where(low, qo > qf, qf > qo)
        first = np.zeros((N, 8, UN), np.int64); n = P
        while n > 1:
            n = n // 2
            swapped = (place >= first[..., None]) & (place < first[..., None] + n)
            a = measure(np.where(swapped, far, own)); b = a[mate]
            s = np.where(low, a > b, b > a)
            first = np.where(s != s0, first, first + n)
        takes = np.where(low, qo < qf, qo <= qf)
        new = np.where(takes[..., None] & (place == first[..., None]), far, own)
        un = np.zeros_like(un); un[n3, g3, order] = new
        A = np.sum(first, axis=2)
    return {"yu": np.stack([gtable(a.reshape(8, -1)) for a in un]).astype(np.float32), "yq": q.astype(np.float32)}

@@ -1,0 +1,572 @@
+from concourse.bass import DstId, RemoteDMATransfer
+from concourse.mybir import AluOpType, AxisListType, ActivationFunctionType
+
+ALU = AluOpType
+ACT = ActivationFunctionType
+BIG = float(1 << 19)
+NC = 3
+CW = 64
+EW = CW * 16
+VG = 32
+UN = 192
+STEP = "pabpcpDpphphp"
+PIECE = {"a": (0, CW // 2), "b": (CW // 2, CW), "c": (0, CW // 2), "D": (CW // 2, CW)}
+
+SCRATCH = {}
+GRAN = {}
+
+
+def _buf(names, cols, dtype, gran=None, where="sbuf"):
+    for name in names.split():
+        SCRATCH[name] = (where, [128, cols], dtype)
+        GRAN[name] = gran if gran else cols
+
+
+_buf("U32", UN, "int32")
+_buf("U16 Uq", UN, "uint16")
+_buf("lu", 4 * UN, "uint16", UN)
+_buf("shelfs", 8192, "bfloat16")
+_buf("Xo Xq Xs Xf V VT sg tk S0A u ks kss yo qs w2", UN, "float32", CW)
+_buf("zi zm ci cj", UN, "int32", CW)
+_buf("off", UN, "uint16", CW)
+_buf("gv mx mn", NC * EW, "bfloat16", 256)
+_buf("B1 B2 B3 B4", UN, "bfloat16", CW)
+_buf("RD", 4 * UN, "bfloat16", CW)
+_buf("lq ly", 4 * UN, "float32", UN)
+_buf("KM Kc", UN, "float32")
+_buf("cmp", 6 * UN, "bfloat16", UN)
+_buf("cmps", 6 * UN, "bfloat16")
+_buf("sj", UN, "bfloat16")
+_buf("acc", 16, "float32", 1)
+_buf("R1 R2", 12, "uint16")
+_buf("Acol", 1, "float32")
+_buf("mmax mmin", EW, "bfloat16")
+_buf("rkm", 6 * UN, "bfloat16")
+_buf("m16 diag uf", UN, "float32")
+_buf("it", UN, "bfloat16")
+_buf("on1", CW, "bfloat16")
+_buf("nhalf", 128, "bfloat16")
+_buf("mm mi mG", 128, "float32")
+_buf("ic", 24, "int32", 1)
+_buf("fc", 72, "float32", 1)
+_buf("SG TR L EQ I16 Lh Eh TRl", 128, "float32")
+for _r in "12":
+    for _n in ("M0", "M1", "Y1", "DP", "SW", "SGX", "EQX", "EQl", "PG"):
+        _buf(_n + _r, 128, "float32")
+    _buf("TWp%s TWn%s" % (_r, _r), 128, "bfloat16")
+_buf("L2 L3 L4 I2 I3 I4", 128, "float32")
+_buf("AW1 AW2 AW3 AW4 KWp KWn QWp QWn", 128, "bfloat16")
+_buf("ZL ZH", 224, "bfloat16")
+_buf("pS0 pS1 pS2 pY0 pY1 pY2 pA pB", 512, "float32", None, "psum")
+PSUM = {n for n in SCRATCH if SCRATCH[n][0] == "psum"}
+SCRATCH["st"] = ("dram", [4, 128, 2048], "bfloat16")
+SCRATCH["rv"] = ("dram", [4, 128, 2048], "bfloat16")
+
+NDMA = 24
+SEMAPHORES = (["cv", "cs", "ct", "cg", "lo", "au", "ad", "aq", "ay"] + ["as%d" % a for a in range(4)]
+              + ["d%d" % k for k in range(NDMA)])
+
+
+def rank_program(g, core, T, topo):
+    rank = T.rank_of(core)
+    if rank is None:
+        return
+    j = rank % 4
+    quad = [T.cores[rank - j + a] for a in range(4)]
+    peers = [j ^ 1, j ^ 2, j ^ 3]
+
+    QUEUE = {"v": g.vector, "s": g.scalar, "t": g.tensor, "g": g, "y": g.sync}
+    SEM = {"v": "cv", "s": "cs", "t": "ct", "g": "cg"}
+    count = {}
+    known = {q: {} for q in QUEUE}
+    state = {}
+
+    def need(q, tok):
+        sem, n, who, clock = tok
+        if known[q].get(sem, 0) >= n:
+            return
+        QUEUE[q].wait_ge(T.sem[sem], n)
+        for s_, v_ in clock.items():
+            if known[q].get(s_, 0) < v_:
+                known[q][s_] = v_
+        known[q][sem] = n
+
+    def entry(k):
+        return state.setdefault(k, {"w": None, "r": {}})
+
+    def emit(q, call, reads=(), writes=(), dma=None):
+        toks = []
+        for ref in reads:
+            for k in ref[1]:
+                e = entry(k)
+                if k[0] in PSUM:
+                    toks += [t for t in e["r"].values() if t[2] != q]
+                if e["w"] and not (k[0] in PSUM and q == "t"):
+                    toks.append(e["w"])
+        for ref in writes:
+            for k in ref[1]:
+                e = entry(k)
+                if k[0] in PSUM:
+                    toks += [t for t in e["r"].values() if t[2] != q or q != "t"]
+                else:
+                    if e["w"]:
+                        toks.append(e["w"])
+                    toks += list(e["r"].values())
+        toks.sort(key=lambda t: -t[1])
+        for t in toks:
+            need(q, t)
+        sem = dma if dma else SEM[q]
+        inc = 16 if dma else 1
+        call().then_inc(T.sem[sem], inc)
+        count[sem] = count.get(sem, 0) + inc
+        tok = (sem, count[sem], None if dma else q, dict(known[q]))
+        for ref in reads:
+            for k in ref[1]:
+                state[k]["r"][sem] = tok
+        for ref in writes:
+            for k in ref[1]:
+                if k[0] in PSUM:
+                    state[k]["r"][sem] = tok
+                    state[k]["w"] = None if q == "t" else tok
+                else:
+                    state[k] = {"w": tok, "r": {}}
+        return tok
+
+    def A(name, lo=0, hi=None, step=None, p0=0, p1=128):
+        hi = SCRATCH[name][1][1] if hi is None else hi
+        ap = T[name][p0:p1, lo:hi] if step is None else T[name][p0:p1, lo:hi:step]
+        gr = GRAN[name]
+        return (ap, [(name, k) for k in range(lo // gr, (hi - 1) // gr + 1)])
+
+    def ind(win, off):
+        return (win[0].indirect(off[0]), win[1] + off[1])
+
+    def val(x):
+        return x[0] if isinstance(x, tuple) else x
+
+    def refs(*xs):
+        return [x for x in xs if isinstance(x, tuple)]
+
+    def tt(out, a, b, op):
+        emit("v", lambda: g.vector.tensor_tensor(out=out[0], in0=a[0], in1=b[0], op=op), [a, b], [out])
+
+    def ts(out, a, s1, op0, s2=None, op1=None):
+        if op1 is None:
+            emit("v", lambda: g.vector.tensor_scalar(out=out[0], in0=a[0], scalar1=val(s1), scalar2=None, op0=op0),
+                 [a] + refs(s1), [out])
+        else:
+            emit("v", lambda: g.vector.tensor_scalar(out=out[0], in0=a[0], scalar1=val(s1), scalar2=val(s2), op0=op0, op1=op1),
+                 [a] + refs(s1, s2), [out])
+
+    def cp(out, a):
+        emit("v", lambda: g.vector.tensor_copy(out=out[0], in_=a[0]), [a], [out])
+
+    def scatter(win, off, a):
+        emit("v", lambda: g.vector.tensor_copy(out=win[0].indirect(off[0]), in_=a[0]), [a, off], [win])
+
+    def fill(out, x):
+        emit("v", lambda: g.vector.memset(out[0], x), [], [out])
+
+    def scan(out, a, b, init, op0, op1):
+        emit("v", lambda: g.vector.tensor_tensor_scan(out=out[0], data0=a[0], data1=b[0], initial=init, op0=op0, op1=op1),
+             [a, b], [out])
+
+    def act(out, a, func, bias=None, scale=None, acc=None):
+        kw = {}
+        if bias is not None:
+            kw["bias"] = val(bias)
+        if scale is not None:
+            kw["scale"] = val(scale)
+        if acc is not None:
+            kw["accum_out"] = acc[0]
+        emit("s", lambda: g.scalar.activation(out=out[0], in_=a[0], func=func, **kw), [a] + refs(bias, scale), [out] + refs(acc))
+
+    def mm(out, lhs, rhs, start=True, stop=True):
+        emit("t", lambda: g.tensor.matmul(out=out[0], lhsT=lhs[0], rhs=rhs[0], start=start, stop=stop), [lhs, rhs], [out])
+
+    ndma = [0]
+
+    def dma(q, out_ap, in_ap, reads=(), writes=()):
+        sem = "d%d" % ndma[0]
+        ndma[0] += 1
+        return emit(q, lambda: QUEUE[q].dma_start(out_ap, in_ap), reads, writes, dma=sem)
+
+    neng = len(topo.engines(core, quad[peers[0]]))
+
+    def fan(src, dst_name, sem):
+        for k in src[1]:
+            need("g", state[k]["w"])
+        ids = []
+        for a in peers:
+            rid, pid, _ = topo.addr(quad[a])
+            ids.append(DstId(rid=rid, pnc=pid))
+        dst = T[dst_name][:, UN * j:UN * j + UN]
+        g.remote_dma_fused([RemoteDMATransfer(dst_ids=ids, dma_engine_mask=topo.mask(core, quad[peers[0]]),
+                                              remote_sem=T.sem[sem], srcs=[src[0]], dsts=[dst, dst, dst])], local_sem=T.sem.lo)
+        count["lo"] = count.get("lo", 0) + neng
+
+    def landed(sem, n, keys):
+        count[sem] = n
+        for k in keys:
+            state[k] = {"w": (sem, n, None, {}), "r": {}}
+
+    def ic(k):
+        return A("ic", k, k + 1)
+
+    def fc(k):
+        return A("fc", k, k + 1)
+
+    dma("y", T.U32[:, :], T.units[:, :], [], [A("U32")])
+    dma("y", T.shelfs[:, :], T.shelf[:, :], [], [A("shelfs")])
+    stage = {}
+    for a in peers:
+        stage[a] = dma("y", T.st[a], T.shelf[32 * a:32 * a + 32, :])
+
+    def iota(ref, pattern, base=0, chan=0):
+        if ref[1][0][0] == "ic":
+            emit("g", lambda: g.iota(ref[0], pattern, base, chan), [], [ref])
+        else:
+            emit("g", lambda: g.iota(ref[0], pattern, base, chan, allow_small_or_imprecise_dtypes=True), [], [ref])
+
+    iota(ic(0), [[0, 1]], 0, 1)
+    iota(A("mi"), [[0, 8], [1, 16]])
+    iota(A("mG"), [[1, 8], [0, 16]])
+    iota(A("mm"), [[1, 128]])
+    cp(A("U16"), A("U32"))
+    fan(A("U16"), "lu", "au")
+    iota(A("uf"), [[0, 12], [1, 16]])
+    iota(A("it"), [[-2, UN]], -2)
+    ts(ic(1), ic(0), 15, ALU.bitwise_and)
+    ts(ic(2), ic(0), 4, ALU.logical_shift_right)
+    for k in range(7):
+        ts(ic(3 + k), ic(0), k, ALU.logical_shift_right, 1, ALU.bitwise_and)
+    cp(A("fc", 0, 10), A("ic", 0, 10))
+    P_, PI, PG_ = fc(0), fc(1), fc(2)
+    ts(A("Xo"), A("U32"), -BIG, ALU.add)
+    ts(A("SG"), A("mG"), PG_, ALU.is_equal)
+    ts(A("TR"), A("mi"), PI, ALU.is_ge)
+    tt(A("L"), A("SG"), A("TR"), ALU.mult)
+    ts(A("EQ"), A("mm"), P_, ALU.is_equal)
+    ts(A("I16"), A("EQ"), 16.0, ALU.mult)
+
+    def cc(name, c):
+        return A(name, CW * c, CW * c + CW)
+
+    def pS(c, k=0):
+        return A("pS%d" % c, CW * k, CW * k + CW)
+
+    def pT(c):
+        return pS(c, 1)
+
+    def pY(c):
+        return A("pY%d" % c, 0, CW)
+
+    def tail(c, mode):
+        if mode is None:
+            tt(cc("zi", c), pS(c), cc("S0A", c), ALU.add)
+        else:
+            ts(cc("zi", c), pS(c), mode, ALU.add)
+        yield
+        ts(cc("zm", c), cc("zi", c), 4095, ALU.bitwise_and)
+        yield
+        tt(cc("w2", c), cc("zm", c), cc("zm", c), ALU.mult)
+        yield
+        tt(cc("ci", c), cc("w2", c), pY(c), ALU.add)
+        yield
+        ts(cc("cj", c), cc("ci", c), 4, ALU.arith_shift_right, 8191, ALU.bitwise_and)
+        yield
+        cp(cc("off", c), cc("cj", c))
+
+    def run(*gens):
+        gens = list(gens)
+        while gens:
+            for x in list(gens):
+                if next(x, 1) == 1:
+                    gens.remove(x)
+
+    def ew(name, c, lo, hi):
+        return A(name, EW * c + 16 * lo, EW * c + 16 * hi)
+
+    def picks(c, lo, hi):
+        return ind(A("shelfs"), A("off", CW * c + lo, CW * c + hi))
+
+    def gather(c, lo=0, hi=CW):
+        act(ew("gv", c, lo, hi), picks(c, lo, hi), ACT.Copy)
+
+    def smax(c, lo=0, hi=CW):
+        scan(ew("mx", c, lo, hi), A("mmax", 0, 16 * (hi - lo)), ew("gv", c, lo, hi), 0.0, ALU.mult, ALU.max)
+
+    def smin(c, lo=0, hi=CW):
+        scan(ew("mn", c, lo, hi), A("mmin", 0, 16 * (hi - lo)), ew("gv", c, lo, hi), 0.0, ALU.add, ALU.min)
+
+    def last(name, c):
+        return A(name, EW * c + 15, EW * c + EW, 16)
+
+    def sums_first(ls, ly, X):
+        for bank, l, c in ((pS, ls, 0), (pS, ls, 1), (pY, ly, 0), (pY, ly, 1), (pS, ls, 2), (pY, ly, 2)):
+            mm(bank(c), l, cc(X, c))
+
+    def measure(X, mode, after):
+        sums_first(A("L"), A("I16"), X)
+        run(tail(0, mode), tail(1, mode))
+        run(tail(2, mode))
+        yield
+        gather(0)
+        gather(1)
+        gather(2, VG, CW)
+        cp(ew("gv", 2, 0, VG), picks(2, 0, VG))
+        smax(2, 0, VG)
+        smin(2, 0, VG)
+        for c in range(2):
+            smax(c)
+            smin(c)
+            after(c)
+        smax(2, VG, CW)
+        smin(2, VG, CW)
+        after(2)
+
+    def mask_fill(name, one, at, step, n):
+        fill(A(name), one)
+        fill(A(name, 0, n, step), at)
+
+    mask_fill("mmax", 1.0, 0.0, 16, EW)
+    mask_fill("mmin", 0.0, 512.0, 16, EW)
+
+    def ranges(c):
+        tt(A("RD", UN * j + CW * c, UN * j + CW * c + CW), last("mx", c), last("mn", c), ALU.subtract)
+
+    m1 = measure("Xo", 0.0, ranges)
+    next(m1)
+
+    def bits(base):
+        return A("fc", base, base + 7)
+    ts(bits(10), bits(3), -1.0, ALU.mult, 1.0, ALU.add)
+    ts(bits(17), bits(3), -2.0, ALU.mult, 1.0, ALU.add)
+    ts(bits(24), bits(3), 2.0, ALU.mult, -1.0, ALU.add)
+    ts(bits(31), bits(10), 16.0, ALU.mult)
+    ts(bits(38), bits(17), 448.0, ALU.mult)
+    ts(bits(45), bits(17), 512.0, ALU.mult)
+    ts(bits(52), bits(24), 512.0, ALU.mult)
+    HI1 = fc(6)
+    LOWC, L16, PBS = ({t: fc(b + 4 - t) for t in (1, 2, 3, 4)} for b in (10, 31, 24))
+    SIDE, NS, THR = ({r: fc(b + 4 + r) for r in (1, 2)} for b in (17, 24, 38))
+    K512, K512N = fc(52 + 6), fc(45 + 6)
+    Z0, Z15, H16, GB = fc(59), fc(60), fc(61), fc(66)
+    ts(Z0, PI, 0.0, ALU.is_equal, -1.0, ALU.mult)
+    ts(Z15, PI, 15.0, ALU.is_equal, fc(10 + 5), ALU.mult)
+    ts(GB, PG_, float(-2 * j), ALU.add)
+    ts(Z15, Z15, 8.0, ALU.mult)
+    ts(H16, HI1, 16.0, ALU.mult)
+    PX, GX = {}, {}
+    for r, X in ((1, 32), (2, 64)):
+        PX[r], GX[r] = fc(61 + r), fc(63 + r)
+        ts(PX[r], SIDE[r], float(X), ALU.mult, P_, ALU.add)
+        ts(GX[r], SIDE[r], X / 16.0, ALU.mult, PG_, ALU.add)
+    for name, x in (("ZL", -512.0), ("ZH", 512.0)):
+        fill(A(name), 0.0)
+        ts(A(name, 96, 128), A("mG", 0, 32), GB, ALU.is_equal, x, ALU.mult)
+    fill(A("on1"), 1.0)
+    ts(A("diag"), A("uf"), PI, ALU.is_equal)
+    mask_fill("m16", 1.0, 0.0, 16, UN)
+    mask_fill("rkm", 1.0, 0.0, UN, 6 * UN)
+    fill(A("nhalf"), -1.0 / 256)
+
+    def scaled(out, a, col):
+        act(A(out), A(a), ACT.Copy, scale=col)
+
+    for t in (2, 3, 4):
+        scaled("L%d" % t, "L", LOWC[t])
+        scaled("I%d" % t, "EQ", L16[t])
+    scaled("Lh", "L", HI1)
+    scaled("Eh", "EQ", H16)
+    scaled("TRl", "TR", LOWC[1])
+    scaled("KWp", "SG", K512)
+    scaled("KWn", "SG", K512N)
+    act(A("QWp"), A("SG"), ACT.Copy)
+    act(A("QWn"), A("SG"), ACT.Copy, scale=-1.0)
+
+    def pass_on(a):
+        need("g", stage[a])
+        rid, pid, _ = topo.addr(quad[a])
+        g.remote_dma(T.rv[j], T.st[a], T.sem["as%d" % j], T.sem.lo, pid, rid, topo.mask(core, quad[a]))
+        count["lo"] += neng
+
+    pass_on(peers[0])
+    pass_on(peers[1])
+    for _ in m1:
+        pass
+    fan(A("RD", UN * j, UN * j + UN), "RD", "ad")
+    pass_on(peers[2])
+
+    for r in (1, 2):
+        ts(A("SGX%d" % r), A("mG"), GX[r], ALU.is_equal)
+        ts(A("EQX%d" % r), A("mm"), PX[r], ALU.is_equal)
+        tt(A("PG%d" % r), A("SG"), A("SGX%d" % r), ALU.add)
+        ts(A("EQl%d" % r), A("EQX%d" % r), L16[1], ALU.mult)
+        tt(A("M0%d" % r), A("SGX%d" % r), A("TRl"), ALU.mult)
+        tt(A("Y1%d" % r), A("EQl%d" % r), A("Eh"), ALU.add)
+        tt(A("M1%d" % r), A("M0%d" % r), A("Lh"), ALU.add)
+        tt(A("DP%d" % r), A("EQX%d" % r), A("EQ"), ALU.subtract)
+        scaled("TWp%d" % r, "PG%d" % r, SIDE[r])
+        scaled("TWn%d" % r, "PG%d" % r, NS[r])
+        scaled("SW%d" % r, "PG%d" % r, Z0)
+        if r == 1:
+            scaled("AW1", "PG1", Z15)
+            for t in (2, 3, 4):
+                act(A("AW%d" % t), A("AW1"), ACT.Copy, scale=2.0 ** (1 - t))
+
+    landed("au", 3 * neng, [("lu", a) for a in peers])
+    for a in range(4):
+        if a == j:
+            src = A("U16", 0, UN, None, 32 * j, 32 * j + 32)
+        else:
+            src = A("lu", UN * a, UN * a + UN, None, 32 * j, 32 * j + 32)
+        dma("y", T.Uq[32 * a:32 * a + 32, :], src[0], [src], [(None, [("Uq4", a)])])
+    own_reads = list(state[("shelfs", 0)]["r"].values())
+    loads = []
+    for a in peers:
+        landed("as%d" % a, neng, [("rv", a)])
+        for t in own_reads:
+            need("y", t)
+        loads.append(dma("y", T.shelfs[32 * a:32 * a + 32, :], T.rv[a], [(None, [("rv", a)])], []))
+    ts(A("Xq"), (T.Uq[:, :], [("Uq4", a) for a in range(4)]), -BIG, ALU.add)
+
+    def iota_row(lo, hi):
+        mm(A("pA", lo, hi), A("nhalf"), A("it", lo, hi), True, False)
+
+    def sort(R):
+        tt(A("KM"), A("pA", 0, UN), A("diag"), ALU.mult)
+        act(A("ks"), A("pA", 0, UN), ACT.Copy)
+        scan(A("Kc"), A("m16"), A("KM"), 0.0, ALU.mult, ALU.add)
+
+        def key(k):
+            return A("Kc", 16 * k + 15, 16 * k + 16)
+        for k in range(6):
+            act(A("sj"), A("ks"), ACT.Sign, bias=key(k), scale=-1.0, acc=A("acc", k, k + 1))
+            ts(A("cmp", UN * k, UN * k + UN), A("ks"), key(6 + k), ALU.is_lt)
+        scan(A("cmps"), A("rkm"), A("cmp"), 0.0, ALU.mult, ALU.add)
+        cp(A(R, 6, 12), A("cmps", UN - 1, 6 * UN, UN))
+        ts(A(R, 0, 6), A("acc", 0, 6), 0.5, ALU.mult, 95.5, ALU.add)
+
+    ones = A("on1")
+
+    def search(r, R, mode, extra):
+        TWp, TWn = A("TWp%d" % r), A("TWn%d" % r)
+        scatter(A("Xs"), A(R), A("Xq"))
+        sums_first(A("M1%d" % r), A("Y1%d" % r), "Xs")
+        mm(A("pB", 0, UN), A("L"), A("Xs"))
+        mm(A("pA", 0, UN), A("DP%d" % r), A("Xs"))
+        if r == 1:
+            for tok in loads:
+                need("s", tok)
+        run(tail(0, mode), tail(1, mode))
+        run(tail(2, mode))
+        for c in range(NC):
+            gather(c)
+        scatter(A("kss"), A(R), A("ks"))
+        ts(A("S0A"), A("pB", 0, UN), mode, ALU.add)
+        cp(A("V"), A("pA", 0, UN))
+        mm(A("pA", UN, 2 * UN), A("SW%d" % r), A("kss"))
+
+        def rest():
+            extra()
+            cp(A("sg"), A("pA", UN, 2 * UN))
+            ts(A("tk"), A("sg"), NS[r], ALU.mult, THR[r], ALU.is_gt)
+
+        def sums(c):
+            mm(pT(c), A("nhalf"), ones, True, False)
+            mm(pT(c), TWp, last("mx", c), False, False)
+            mm(pT(c), TWn, last("mn", c), False, True)
+
+        def keep(c, t):
+            tt(cc("u", c), pT(c), cc("sg", c), ALU.mult)
+            yield
+            bt = cc("B%d" % t, c) if r == 1 else pS(c, 2)
+            ts(bt, cc("u", c), PBS[t], ALU.mult, 0.0, ALU.is_gt)
+            yield
+            if t == 4:
+                tt(pS(c, 3), bt, cc("VT", c), ALU.mult)
+                yield
+                tt(cc("Xf", c), pS(c, 3), cc("Xs", c), ALU.add)
+                return
+            tt(cc("V", c), bt, cc("V", c), ALU.mult)
+            mm(pS(c), A("L%d" % (t + 1)), cc("V", c))
+            mm(pY(c), A("I16"), cc("Xs", c), True, False)
+            mm(pY(c), A("I%d" % (t + 1)), cc("V", c), False, True)
+            yield
+            if t == 3:
+                tt(cc("VT", c), cc("tk", c), cc("V", c), ALU.mult)
+            for _ in tail(c, None):
+                yield
+            gather(c)
+
+        before = iter(())
+        for t in (1, 2, 3, 4):
+            for c in range(NC):
+                now = keep(c, t)
+                for x in STEP:
+                    if x == "p":
+                        next(before, None)
+                    elif x == "h":
+                        if rest:
+                            rest()
+                            rest = None
+                        next(now)
+                    else:
+                        (smax if x in "ab" else smin)(c, *PIECE[x])
+                        if x == "D":
+                            sums(c)
+                run(before)
+                before = now
+        if r == 1:
+            for t in (1, 2, 3, 4):
+                mm(A("pA", 0, UN), A("AW%d" % t), A("B%d" % t), t == 1, t == 4)
+        run(before)
+
+    landed("ad", 3 * neng, [("RD", 3 * a + c) for a in peers for c in range(3)])
+    iota_row(0, UN)
+    for n, a in enumerate([j] + peers):
+        z = A("ZL" if a % 2 == 0 else "ZH", 96 - 32 * a, 224 - 32 * a)
+        mm(A("pA", 0, UN), z, A("RD", UN * a, UN * a + UN), False, n == 3)
+    sort("R1")
+    search(1, "R1", 0.0, lambda: None)
+    cp(A("Xq"), ind(A("Xf"), A("R1")))
+    emit("v", lambda: g.vector.tensor_reduce(out=T.Acol[:, :], in_=A("pA", 0, UN)[0], axis=AxisListType.X, op=ALU.add),
+         [A("pA", 0, UN)], [A("Acol")])
+
+    def keys2(c):
+        lo, hi = CW * c, CW * c + CW
+        iota_row(lo, hi)
+        mm(A("pA", lo, hi), A("KWp"), last("mx", c), False, False)
+        mm(A("pA", lo, hi), A("KWn"), last("mn", c), False, True)
+
+    for _ in measure("Xq", A("Acol"), keys2):
+        pass
+    sort("R2")
+    for c in range(NC):
+        q_ = A("pB", UN + CW * c, UN + CW * c + CW)
+        mm(q_, A("QWp"), last("mx", c), True, False)
+        mm(q_, A("QWn"), last("mn", c), False, True)
+
+    def send_q():
+        cp(A("qs"), A("pB", UN, 2 * UN))
+        fan(A("qs"), "lq", "aq")
+
+    search(2, "R2", A("Acol"), send_q)
+
+    landed("aq", 3 * neng, [("lq", a) for a in peers])
+    for a in [j] + peers:
+        lo = 0 if a == j else UN * a
+        name = "qs" if a == j else "lq"
+        src = A(name, lo, lo + UN)
+        dma("y", T.yq[2 * a:2 * a + 2, :], T[name][32 * j:32 * j + 32:16, lo:lo + UN], [src])
+    ts(A("yo"), ind(A("Xf"), A("R2")), BIG, ALU.add)
+    fan(A("yo"), "ly", "ay")
+    landed("ay", 3 * neng, [("ly", a) for a in peers])
+    for n, a in enumerate([j] + peers):
+        lo = 0 if a == j else UN * a
+        src = A("yo" if a == j else "ly", lo, lo + UN, None, 32 * j, 32 * j + 32)
+        dma("s" if n % 2 else "y", T.yu[32 * a:32 * a + 32, :], src[0], [src])
+    for sem, n in sorted(count.items()):
+        if known["y"].get(sem, 0) < n:
+            g.sync.wait_ge(T.sem[sem], n)

@@ -3,14 +3,17 @@ from concourse.mybir import AluOpType, AxisListType, ActivationFunctionType
 
 ALU = AluOpType
 ACT = ActivationFunctionType
-BIG = float(1 << 19)
+UN = 192
 NC = 3
 CW = 64
-EW = CW * 16
-VG = 32
-UN = 192
-STEP = "pabpcpDpphphp"
-PIECE = {"a": (0, CW // 2), "b": (CW // 2, CW), "c": (0, CW // 2), "D": (CW // 2, CW)}
+GS = 32
+LIFT = 160 * 4096.0
+BAND = 1.5 * 2.0 ** 36
+SLOT = "A0 g2 r1 B0 q1 G2 d0 f1 e0 h1 k1"
+M1_S, M1_V = (64, 64, 32, 16), 16
+M2_S, M2_V = (32, 64, 64, 16), 16
+SORT_S = 7
+EARLY = 6144
 
 SCRATCH = {}
 GRAN = {}
@@ -23,39 +26,38 @@ def _buf(names, cols, dtype, gran=None, where="sbuf"):
 
 
 _buf("U32", UN, "int32")
-_buf("U16 Uq", UN, "uint16")
-_buf("lu", 4 * UN, "uint16", UN)
-_buf("shelfs", 8192, "bfloat16")
-_buf("Xo Xq Xs Xf V VT sg tk S0A u ks kss yo qs w2", UN, "float32", CW)
-_buf("zi zm ci cj", UN, "int32", CW)
-_buf("off", UN, "uint16", CW)
-_buf("gv mx mn", NC * EW, "bfloat16", 256)
-_buf("B1 B2 B3 B4", UN, "bfloat16", CW)
-_buf("RD", 4 * UN, "bfloat16", CW)
+_buf("lu", 4 * UN, "float32", UN)
+_buf("shelfs", 8192, "bfloat16", 2048)
+_buf("Xo Xq Xn Xs V ks kss yo qs w2", UN, "float32", 16)
+_buf("ci cj", UN, "int32", 16)
+_buf("off", UN, "uint16", 16)
+_buf("gv mx mn", UN * 16, "bfloat16", 256)
+_buf("B1 B2 B3 B4 rq sg tk stk", UN, "bfloat16", 16)
+_buf("RD", 4 * UN, "bfloat16", 16)
 _buf("lq ly", 4 * UN, "float32", UN)
 _buf("KM Kc", UN, "float32")
 _buf("cmp", 6 * UN, "bfloat16", UN)
 _buf("cmps", 6 * UN, "bfloat16")
-_buf("sj", UN, "bfloat16")
+_buf("sj", 12 * UN, "bfloat16", UN)
 _buf("acc", 16, "float32", 1)
-_buf("R1 R2", 12, "uint16")
-_buf("Acol", 1, "float32")
-_buf("mmax mmin", EW, "bfloat16")
+_buf("R1 R2", 12, "uint16", 1)
+_buf("Acol", 4, "float32", 1)
+_buf("mmax mmin", CW * 16, "bfloat16")
 _buf("rkm", 6 * UN, "bfloat16")
 _buf("m16 diag uf", UN, "float32")
-_buf("it", UN, "bfloat16")
-_buf("on1", CW, "bfloat16")
-_buf("nhalf", 128, "bfloat16")
-_buf("mm mi mG", 128, "float32")
+_buf("it on1 big", UN, "bfloat16")
+_buf("ones", 6 * UN, "bfloat16")
+_buf("nhalf RM", 128, "bfloat16")
+_buf("mm mi mG mP1 mP2", 128, "float32", 64)
 _buf("ic", 24, "int32", 1)
-_buf("fc", 72, "float32", 1)
-_buf("SG TR L EQ I16 Lh Eh TRl", 128, "float32")
+_buf("fc", 96, "float32", 1)
+_buf("SG TR L NEQ I16", 128, "float32")
 for _r in "12":
-    for _n in ("M0", "M1", "Y1", "DP", "SW", "SGX", "EQX", "EQl", "PG"):
+    for _n in ("M0", "M1", "Y1", "DP", "SW", "PG"):
         _buf(_n + _r, 128, "float32")
     _buf("TWp%s TWn%s" % (_r, _r), 128, "bfloat16")
 _buf("L2 L3 L4 I2 I3 I4", 128, "float32")
-_buf("AW1 AW2 AW3 AW4 KWp KWn QWp QWn", 128, "bfloat16")
+_buf("AW1 AW2 AW3 AW4 CP1 CP2 CP3 CP4 KWp KWn", 128, "bfloat16")
 _buf("ZL ZH", 224, "bfloat16")
 _buf("pS0 pS1 pS2 pY0 pY1 pY2 pA pB", 512, "float32", None, "psum")
 PSUM = {n for n in SCRATCH if SCRATCH[n][0] == "psum"}
@@ -63,7 +65,7 @@ SCRATCH["st"] = ("dram", [4, 128, 2048], "bfloat16")
 SCRATCH["rv"] = ("dram", [4, 128, 2048], "bfloat16")
 
 NDMA = 24
-SEMAPHORES = (["cv", "cs", "ct", "cg", "lo", "au", "ad", "aq", "ay"] + ["as%d" % a for a in range(4)]
+SEMAPHORES = (["cv", "cs", "ct", "cg", "lo", "lr", "au", "ad", "aq", "ay"] + ["as%d" % a for a in range(4)]
               + ["d%d" % k for k in range(NDMA)])
 
 
@@ -184,6 +186,15 @@ def rank_program(g, core, T, topo):
     def mm(out, lhs, rhs, start=True, stop=True):
         emit("t", lambda: g.tensor.matmul(out=out[0], lhsT=lhs[0], rhs=rhs[0], start=start, stop=stop), [lhs, rhs], [out])
 
+    def iota(ref, pattern, base=0, chan=0):
+        if ref[1][0][0] == "ic":
+            emit("g", lambda: g.iota(ref[0], pattern, base, chan), [], [ref])
+        else:
+            emit("g", lambda: g.iota(ref[0], pattern, base, chan, allow_small_or_imprecise_dtypes=True), [], [ref])
+
+    def select(out, a, pattern, op, x, base=0, chan=0):
+        emit("g", lambda: g.affine_select(out[0], a[0], pattern, op, x, base, chan), [a], [out])
+
     ndma = [0]
 
     def dma(q, out_ap, in_ap, reads=(), writes=()):
@@ -193,7 +204,7 @@ def rank_program(g, core, T, topo):
 
     neng = len(topo.engines(core, quad[peers[0]]))
 
-    def fan(src, dst_name, sem):
+    def fan(src, dst_name, sem, left="lo"):
         for k in src[1]:
             need("g", state[k]["w"])
         ids = []
@@ -202,8 +213,8 @@ def rank_program(g, core, T, topo):
             ids.append(DstId(rid=rid, pnc=pid))
         dst = T[dst_name][:, UN * j:UN * j + UN]
         g.remote_dma_fused([RemoteDMATransfer(dst_ids=ids, dma_engine_mask=topo.mask(core, quad[peers[0]]),
-                                              remote_sem=T.sem[sem], srcs=[src[0]], dsts=[dst, dst, dst])], local_sem=T.sem.lo)
-        count["lo"] = count.get("lo", 0) + neng
+                                              remote_sem=T.sem[sem], srcs=[src[0]], dsts=[dst, dst, dst])], local_sem=T.sem[left])
+        count[left] = count.get(left, 0) + neng
 
     def landed(sem, n, keys):
         count[sem] = n
@@ -217,173 +228,178 @@ def rank_program(g, core, T, topo):
         return A("fc", k, k + 1)
 
     dma("y", T.U32[:, :], T.units[:, :], [], [A("U32")])
-    dma("y", T.shelfs[:, :], T.shelf[:, :], [], [A("shelfs")])
+    early = dma("y", T.shelfs[:, :EARLY], T.shelf[:, :EARLY], [], [A("shelfs", 0, EARLY)])
+    dma("y", T.shelfs[:, EARLY:], T.shelf[:, EARLY:], [], [A("shelfs", EARLY)])
+    need("y", early)
     stage = {}
     for a in peers:
         stage[a] = dma("y", T.st[a], T.shelf[32 * a:32 * a + 32, :])
-
-    def iota(ref, pattern, base=0, chan=0):
-        if ref[1][0][0] == "ic":
-            emit("g", lambda: g.iota(ref[0], pattern, base, chan), [], [ref])
-        else:
-            emit("g", lambda: g.iota(ref[0], pattern, base, chan, allow_small_or_imprecise_dtypes=True), [], [ref])
 
     iota(ic(0), [[0, 1]], 0, 1)
     iota(A("mi"), [[0, 8], [1, 16]])
     iota(A("mG"), [[1, 8], [0, 16]])
     iota(A("mm"), [[1, 128]])
-    cp(A("U16"), A("U32"))
-    fan(A("U16"), "lu", "au")
-    iota(A("uf"), [[0, 12], [1, 16]])
-    iota(A("it"), [[-2, UN]], -2)
+    fill(A("ones"), 1.0)
+    fill(A("nhalf"), -1.0 / 256)
+    fill(A("big"), 2.0 ** 24)
     ts(ic(1), ic(0), 15, ALU.bitwise_and)
     ts(ic(2), ic(0), 4, ALU.logical_shift_right)
     for k in range(7):
         ts(ic(3 + k), ic(0), k, ALU.logical_shift_right, 1, ALU.bitwise_and)
     cp(A("fc", 0, 10), A("ic", 0, 10))
     P_, PI, PG_ = fc(0), fc(1), fc(2)
-    ts(A("Xo"), A("U32"), -BIG, ALU.add)
-    ts(A("SG"), A("mG"), PG_, ALU.is_equal)
     ts(A("TR"), A("mi"), PI, ALU.is_ge)
+    cp(A("Xo"), A("U32"))
+    ts(A("SG"), A("mG"), PG_, ALU.is_equal)
+    ts(A("NEQ"), A("mm"), P_, ALU.is_equal, -1.0, ALU.mult)
     tt(A("L"), A("SG"), A("TR"), ALU.mult)
-    ts(A("EQ"), A("mm"), P_, ALU.is_equal)
-    ts(A("I16"), A("EQ"), 16.0, ALU.mult)
+    fan(A("Xo"), "lu", "au")
+    act(A("I16"), A("NEQ"), ACT.Copy, scale=-16.0)
+    act(A("RM"), A("NEQ"), ACT.Copy, scale=4096.0)
 
-    def cc(name, c):
-        return A(name, CW * c, CW * c + CW)
-
-    def pS(c, k=0):
-        return A("pS%d" % c, CW * k, CW * k + CW)
+    def pS(c, n=CW):
+        return A("pS%d" % c, 0, n)
 
     def pT(c):
-        return pS(c, 1)
+        return A("pS%d" % c, UN, UN + CW)
 
-    def pY(c):
-        return A("pY%d" % c, 0, CW)
+    def pY(c, n=CW):
+        return A("pY%d" % c, 0, n)
 
-    def tail(c, mode):
-        if mode is None:
-            tt(cc("zi", c), pS(c), cc("S0A", c), ALU.add)
-        else:
-            ts(cc("zi", c), pS(c), mode, ALU.add)
-        yield
-        ts(cc("zm", c), cc("zi", c), 4095, ALU.bitwise_and)
-        yield
-        tt(cc("w2", c), cc("zm", c), cc("zm", c), ALU.mult)
-        yield
-        tt(cc("ci", c), cc("w2", c), pY(c), ALU.add)
-        yield
-        ts(cc("cj", c), cc("ci", c), 4, ALU.arith_shift_right, 8191, ALU.bitwise_and)
-        yield
-        cp(cc("off", c), cc("cj", c))
+    def tail(c, z, lo, hi, lift):
+        def r():
+            ts(A("rq", lo, hi), pS(c, hi - lo), lift[0], ALU.add, 2.0 ** -12, ALU.mult)
+            mm(z, A("RM"), A("rq", lo, hi), False, True)
+        return {"r": r,
+                "q": lambda: act(A("w2", lo, hi), z, ACT.Square, bias=lift[1]),
+                "f": lambda: tt(A("ci", lo, hi), A("w2", lo, hi), pY(c, hi - lo), ALU.add),
+                "h": lambda: ts(A("cj", lo, hi), A("ci", lo, hi), 4, ALU.arith_shift_right, 8191, ALU.bitwise_and),
+                "k": lambda: cp(A("off", lo, hi), A("cj", lo, hi))}
 
-    def run(*gens):
-        gens = list(gens)
-        while gens:
-            for x in list(gens):
-                if next(x, 1) == 1:
-                    gens.remove(x)
+    def columns(ls, ly, X, cut, lift, between=None):
+        parts = [(c, lo, hi) for c, (lo, hi) in enumerate(((0, cut), (cut, UN))) if hi > lo]
+        for c, lo, hi in parts:
+            mm(pY(c, hi - lo), A("nhalf"), A("big", lo, hi), True, False)
+        for c, lo, hi in parts:
+            mm(pS(c, hi - lo), ls, A(X, lo, hi))
+            mm((pS, pY)[c](2, hi - lo), ls, A(X, lo, hi), True, False)
+        for c, lo, hi in parts:
+            mm(pY(c, hi - lo), ly, A(X, lo, hi), False, True)
+        calls = [tail(c, (pS, pY)[c](2, hi - lo), lo, hi, lift) for c, lo, hi in parts]
+        for x in "rq":
+            for t in calls:
+                t[x]()
+        if between:
+            between()
+        for t in calls:
+            for x in "fhk":
+                t[x]()
 
-    def ew(name, c, lo, hi):
-        return A(name, EW * c + 16 * lo, EW * c + 16 * hi)
+    def ew(name, lo, hi):
+        return A(name, 16 * lo, 16 * hi)
 
-    def picks(c, lo, hi):
-        return ind(A("shelfs"), A("off", CW * c + lo, CW * c + hi))
+    def picks(lo, hi):
+        return ind(A("shelfs"), A("off", lo, hi))
 
-    def gather(c, lo=0, hi=CW):
-        act(ew("gv", c, lo, hi), picks(c, lo, hi), ACT.Copy)
+    def gather(lo, hi):
+        act(ew("gv", lo, hi), picks(lo, hi), ACT.Copy)
 
-    def smax(c, lo=0, hi=CW):
-        scan(ew("mx", c, lo, hi), A("mmax", 0, 16 * (hi - lo)), ew("gv", c, lo, hi), 0.0, ALU.mult, ALU.max)
+    def smax(lo, hi):
+        scan(ew("mx", lo, hi), A("mmax", 0, 16 * (hi - lo)), ew("gv", lo, hi), 0.0, ALU.mult, ALU.max)
 
-    def smin(c, lo=0, hi=CW):
-        scan(ew("mn", c, lo, hi), A("mmin", 0, 16 * (hi - lo)), ew("gv", c, lo, hi), 0.0, ALU.add, ALU.min)
+    def smin(lo, hi):
+        scan(ew("mn", lo, hi), A("mmin", 0, 16 * (hi - lo)), ew("gv", lo, hi), 0.0, ALU.add, ALU.min)
 
-    def last(name, c):
-        return A(name, EW * c + 15, EW * c + EW, 16)
+    def last(name, lo, hi):
+        return A(name, 16 * lo + 15, 16 * hi, 16)
 
-    def sums_first(ls, ly, X):
-        for bank, l, c in ((pS, ls, 0), (pS, ls, 1), (pY, ly, 0), (pY, ly, 1), (pS, ls, 2), (pY, ly, 2)):
-            mm(bank(c), l, cc(X, c))
+    def measure(pieces, own, after):
+        cuts = [sum(pieces[:k]) for k in range(len(pieces) + 1)]
+        for lo, hi in zip(cuts, cuts[1:]):
+            gather(lo, hi)
+        order = list(zip(cuts, cuts[1:]))
+        if own:
+            cp(ew("gv", UN - own, UN), picks(UN - own, UN))
+            order = [(UN - own, UN)] + order
+        for lo, hi in order:
+            smax(lo, hi)
+            smin(lo, hi)
+            after(lo, hi)
 
-    def measure(X, mode, after):
-        sums_first(A("L"), A("I16"), X)
-        run(tail(0, mode), tail(1, mode))
-        run(tail(2, mode))
-        yield
-        gather(0)
-        gather(1)
-        gather(2, VG, CW)
-        cp(ew("gv", 2, 0, VG), picks(2, 0, VG))
-        smax(2, 0, VG)
-        smin(2, 0, VG)
-        for c in range(2):
-            smax(c)
-            smin(c)
-            after(c)
-        smax(2, VG, CW)
-        smin(2, VG, CW)
-        after(2)
+    LC = fc(90)
+    fill(LC, LIFT)
+    lift1 = (LIFT - 2047.5, LC)
+    columns(A("L"), A("I16"), "Xo", UN, lift1)
 
     def mask_fill(name, one, at, step, n):
         fill(A(name), one)
         fill(A(name, 0, n, step), at)
 
-    mask_fill("mmax", 1.0, 0.0, 16, EW)
-    mask_fill("mmin", 0.0, 512.0, 16, EW)
+    mask_fill("mmax", 1.0, 0.0, 16, 16 * CW)
+    mask_fill("mmin", 0.0, 512.0, 16, 16 * CW)
 
-    def ranges(c):
-        tt(A("RD", UN * j + CW * c, UN * j + CW * c + CW), last("mx", c), last("mn", c), ALU.subtract)
-
-    m1 = measure("Xo", 0.0, ranges)
-    next(m1)
+    iota(A("uf"), [[0, 12], [1, 16]])
+    iota(A("it"), [[-2, UN]], -2)
+    for h in (0, 1):
+        iota(A("mP1", 64 * h, 64 * h + 64), [[0, 2], [1, 2], [0, 16]], 4 * h)
+    iota(A("mP2"), [[0, 2], [1, 4], [0, 16]])
+    select(A("DP1"), A("NEQ"), [[-64, 2], [32, 2], [-1, 32]], ALU.not_equal, 1.0, -32, 1)
 
     def bits(base):
         return A("fc", base, base + 7)
     ts(bits(10), bits(3), -1.0, ALU.mult, 1.0, ALU.add)
     ts(bits(17), bits(3), -2.0, ALU.mult, 1.0, ALU.add)
     ts(bits(24), bits(3), 2.0, ALU.mult, -1.0, ALU.add)
-    ts(bits(31), bits(10), 16.0, ALU.mult)
+    ts(bits(31), bits(10), -16.0, ALU.mult)
     ts(bits(38), bits(17), 448.0, ALU.mult)
     ts(bits(45), bits(17), 512.0, ALU.mult)
     ts(bits(52), bits(24), 512.0, ALU.mult)
-    HI1 = fc(6)
-    LOWC, L16, PBS = ({t: fc(b + 4 - t) for t in (1, 2, 3, 4)} for b in (10, 31, 24))
+    ts(bits(59), bits(17), 8192.0, ALU.mult)
+    LOWC, L16, PB = ({t: fc(b + 4 - t) for t in (1, 2, 3, 4)} for b in (10, 31, 59))
     SIDE, NS, THR = ({r: fc(b + 4 + r) for r in (1, 2)} for b in (17, 24, 38))
     K512, K512N = fc(52 + 6), fc(45 + 6)
-    Z0, Z15, H16, GB = fc(59), fc(60), fc(61), fc(66)
+    Z0, Z15, Z15L, GB, QS = fc(66), fc(67), fc(68), fc(69), fc(70)
     ts(Z0, PI, 0.0, ALU.is_equal, -1.0, ALU.mult)
-    ts(Z15, PI, 15.0, ALU.is_equal, fc(10 + 5), ALU.mult)
+    ts(Z15, PI, 15.0, ALU.is_equal)
     ts(GB, PG_, float(-2 * j), ALU.add)
-    ts(Z15, Z15, 8.0, ALU.mult)
-    ts(H16, HI1, 16.0, ALU.mult)
-    PX, GX = {}, {}
-    for r, X in ((1, 32), (2, 64)):
-        PX[r], GX[r] = fc(61 + r), fc(63 + r)
-        ts(PX[r], SIDE[r], float(X), ALU.mult, P_, ALU.add)
-        ts(GX[r], SIDE[r], X / 16.0, ALU.mult, PG_, ALU.add)
-    for name, x in (("ZL", -512.0), ("ZH", 512.0)):
-        fill(A(name), 0.0)
-        ts(A(name, 96, 128), A("mG", 0, 32), GB, ALU.is_equal, x, ALU.mult)
-    fill(A("on1"), 1.0)
-    ts(A("diag"), A("uf"), PI, ALU.is_equal)
-    mask_fill("m16", 1.0, 0.0, 16, UN)
-    mask_fill("rkm", 1.0, 0.0, UN, 6 * UN)
-    fill(A("nhalf"), -1.0 / 256)
+    ts(QS, NS[2], 1.0 / 512, ALU.mult)
+    ts(Z15L, Z15, fc(10 + 5), ALU.mult, 8.0, ALU.mult)
+    SRC, GRP, PAIR = {}, {}, {}
+    for r, X in ((1, 32.0), (2, 64.0)):
+        SRC[r], GRP[r], PAIR[r] = fc(71 + r), fc(74 + r), fc(77 + r)
+        ts(fc(80 + r), SIDE[r], LOWC[1], ALU.mult)
+        ts(PAIR[r], fc(7 + r), -X / 16, ALU.mult, PG_, ALU.add)
+    for r, X in ((1, 32.0), (2, 64.0)):
+        ts(SRC[r], fc(80 + r), X, ALU.mult, P_, ALU.add)
+        ts(GRP[r], fc(80 + r), X / 16, ALU.mult, PG_, ALU.add)
 
     def scaled(out, a, col):
         act(A(out), A(a), ACT.Copy, scale=col)
 
+    def pair_matrices(r):
+        ts(A("M0%d" % r), A("mG"), GRP[r], ALU.is_equal)
+        ts(A("PG%d" % r), A("mP%d" % r), PAIR[r], ALU.is_equal)
+        ts(A("Y1%d" % r), A("mm"), SRC[r], ALU.is_equal, 16.0, ALU.mult)
+        tt(A("M1%d" % r), A("M0%d" % r), A("TR"), ALU.mult)
+
+    def pair_scaled(r):
+        scaled("TWp%d" % r, "PG%d" % r, SIDE[r])
+        scaled("TWn%d" % r, "PG%d" % r, NS[r])
+        scaled("SW%d" % r, "PG%d" % r, Z0)
+
     for t in (2, 3, 4):
         scaled("L%d" % t, "L", LOWC[t])
-        scaled("I%d" % t, "EQ", L16[t])
-    scaled("Lh", "L", HI1)
-    scaled("Eh", "EQ", H16)
-    scaled("TRl", "TR", LOWC[1])
+        scaled("I%d" % t, "NEQ", L16[t])
+    for t in (1, 2, 3, 4):
+        scaled("CP%d" % t, "NEQ", PB[t])
     scaled("KWp", "SG", K512)
     scaled("KWn", "SG", K512N)
-    act(A("QWp"), A("SG"), ACT.Copy)
-    act(A("QWn"), A("SG"), ACT.Copy, scale=-1.0)
+    fill(A("ZL"), 0.0)
+    ts(A("diag"), A("uf"), PI, ALU.is_equal)
+    ts(A("ZL", 96, 128), A("mG", 0, 32), GB, ALU.is_equal, -512.0, ALU.mult)
+    ts(A("m16"), A("uf"), 0.0, ALU.is_gt)
+    pair_matrices(1)
+    act(A("ZH"), A("ZL"), ACT.Copy, scale=-1.0)
 
     def pass_on(a):
         need("g", stage[a])
@@ -391,168 +407,176 @@ def rank_program(g, core, T, topo):
         g.remote_dma(T.rv[j], T.st[a], T.sem["as%d" % j], T.sem.lo, pid, rid, topo.mask(core, quad[a]))
         count["lo"] += neng
 
-    pass_on(peers[0])
-    pass_on(peers[1])
-    for _ in m1:
-        pass
-    fan(A("RD", UN * j, UN * j + UN), "RD", "ad")
-    pass_on(peers[2])
+    def ranges(lo, hi):
+        tt(A("RD", UN * j + lo, UN * j + hi), last("mx", lo, hi), last("mn", lo, hi), ALU.subtract)
 
-    for r in (1, 2):
-        ts(A("SGX%d" % r), A("mG"), GX[r], ALU.is_equal)
-        ts(A("EQX%d" % r), A("mm"), PX[r], ALU.is_equal)
-        tt(A("PG%d" % r), A("SG"), A("SGX%d" % r), ALU.add)
-        ts(A("EQl%d" % r), A("EQX%d" % r), L16[1], ALU.mult)
-        tt(A("M0%d" % r), A("SGX%d" % r), A("TRl"), ALU.mult)
-        tt(A("Y1%d" % r), A("EQl%d" % r), A("Eh"), ALU.add)
-        tt(A("M1%d" % r), A("M0%d" % r), A("Lh"), ALU.add)
-        tt(A("DP%d" % r), A("EQX%d" % r), A("EQ"), ALU.subtract)
-        scaled("TWp%d" % r, "PG%d" % r, SIDE[r])
-        scaled("TWn%d" % r, "PG%d" % r, NS[r])
-        scaled("SW%d" % r, "PG%d" % r, Z0)
-        if r == 1:
-            scaled("AW1", "PG1", Z15)
-            for t in (2, 3, 4):
-                act(A("AW%d" % t), A("AW1"), ACT.Copy, scale=2.0 ** (1 - t))
+    todo = []
+
+    def ranges_late(lo, hi):
+        todo.append((lo, hi))
+        if hi == UN - M1_V - M1_S[-1]:
+            ranges(0, hi)
+        if hi == UN - M1_V:
+            ranges(lo, UN)
+
+    pass_on(peers[0])
+    select(A("rkm", 0, (12 - SORT_S) * UN), A("ones", 0, (12 - SORT_S) * UN), [[0, 12 - SORT_S], [1, UN]], ALU.is_gt, 0.0)
+    pass_on(peers[1])
+    measure(M1_S, M1_V, ranges_late)
+    fan(A("RD", UN * j, UN * j + UN), "RD", "ad", "lr")
+    pass_on(peers[2])
+    select(A("DP2"), A("NEQ"), [[64, 2], [-1, 64]], ALU.not_equal, 1.0, -64, 1)
+
+    pair_matrices(2)
+    pair_scaled(1)
+    scaled("AW1", "PG1", Z15L)
+    scaled("AW4", "PG1", Z15)
+    for t in (2, 3):
+        act(A("AW%d" % t), A("AW1"), ACT.Copy, scale=2.0 ** (1 - t))
+    pair_scaled(2)
 
     landed("au", 3 * neng, [("lu", a) for a in peers])
     for a in range(4):
-        if a == j:
-            src = A("U16", 0, UN, None, 32 * j, 32 * j + 32)
-        else:
-            src = A("lu", UN * a, UN * a + UN, None, 32 * j, 32 * j + 32)
-        dma("y", T.Uq[32 * a:32 * a + 32, :], src[0], [src], [(None, [("Uq4", a)])])
+        src = A("Xo", 0, UN, None, 32 * j, 32 * j + 32) if a == j else A("lu", UN * a, UN * a + UN, None, 32 * j, 32 * j + 32)
+        dma("y", T.Xq[32 * a:32 * a + 32, :], src[0], [src], [(None, [("Xq4", a)])])
+    Xq = (T.Xq[:, :], [("Xq4", a) for a in range(4)])
     own_reads = list(state[("shelfs", 0)]["r"].values())
     loads = []
+    need("y", ("lr", neng, None, {}))
     for a in peers:
         landed("as%d" % a, neng, [("rv", a)])
         for t in own_reads:
             need("y", t)
         loads.append(dma("y", T.shelfs[32 * a:32 * a + 32, :], T.rv[a], [(None, [("rv", a)])], []))
-    ts(A("Xq"), (T.Uq[:, :], [("Uq4", a) for a in range(4)]), -BIG, ALU.add)
 
-    def iota_row(lo, hi):
-        mm(A("pA", lo, hi), A("nhalf"), A("it", lo, hi), True, False)
+    def iota_row(bank):
+        mm(A(bank, 0, UN), A("nhalf"), A("it"), True, False)
 
     def sort(R):
+        nv = 12 - SORT_S
         tt(A("KM"), A("pA", 0, UN), A("diag"), ALU.mult)
-        act(A("ks"), A("pA", 0, UN), ACT.Copy)
+        act(A("ks"), A("pB", 0, UN), ACT.Copy)
         scan(A("Kc"), A("m16"), A("KM"), 0.0, ALU.mult, ALU.add)
 
         def key(k):
             return A("Kc", 16 * k + 15, 16 * k + 16)
-        for k in range(6):
-            act(A("sj"), A("ks"), ACT.Sign, bias=key(k), scale=-1.0, acc=A("acc", k, k + 1))
-            ts(A("cmp", UN * k, UN * k + UN), A("ks"), key(6 + k), ALU.is_lt)
-        scan(A("cmps"), A("rkm"), A("cmp"), 0.0, ALU.mult, ALU.add)
-        cp(A(R, 6, 12), A("cmps", UN - 1, 6 * UN, UN))
-        ts(A(R, 0, 6), A("acc", 0, 6), 0.5, ALU.mult, 95.5, ALU.add)
+        for k in range(SORT_S):
+            act(A("sj", UN * k, UN * k + UN), A("ks"), ACT.Sign, bias=key(k), scale=-1.0, acc=A("acc", k, k + 1))
+        for k in range(nv):
+            ts(A("cmp", UN * k, UN * k + UN), A("ks"), key(SORT_S + k), ALU.is_lt)
+        scan(A("cmps", 0, nv * UN), A("rkm", 0, nv * UN), A("cmp", 0, nv * UN), 0.0, ALU.mult, ALU.add)
+        cp(A(R, SORT_S, 12), A("cmps", UN - 1, nv * UN, UN))
+        ts(A(R, 0, SORT_S), A("acc", 0, SORT_S), 0.5, ALU.mult, 95.5, ALU.add)
 
-    ones = A("on1")
-
-    def search(r, R, mode, extra):
+    def search(r, R, X, lift, extra):
         TWp, TWn = A("TWp%d" % r), A("TWn%d" % r)
-        scatter(A("Xs"), A(R), A("Xq"))
-        sums_first(A("M1%d" % r), A("Y1%d" % r), "Xs")
-        mm(A("pB", 0, UN), A("L"), A("Xs"))
-        mm(A("pA", 0, UN), A("DP%d" % r), A("Xs"))
+        scatter(A("Xs"), A(R), X)
+
+        def suspects():
+            mm(A("pA", 0, UN), A("DP%d" % r), A("Xs"))
+            act(A("V"), A("pA", 0, UN), ACT.Copy)
+        columns(A("M1%d" % r), A("Y1%d" % r), "Xs", CW, lift, suspects)
         if r == 1:
             for tok in loads:
                 need("s", tok)
-        run(tail(0, mode), tail(1, mode))
-        run(tail(2, mode))
-        for c in range(NC):
-            gather(c)
         scatter(A("kss"), A(R), A("ks"))
-        ts(A("S0A"), A("pB", 0, UN), mode, ALU.add)
-        cp(A("V"), A("pA", 0, UN))
-        mm(A("pA", UN, 2 * UN), A("SW%d" % r), A("kss"))
+        mm(A("pB", 0, UN), A("SW%d" % r), A("kss"))
+        extra()
+        ts(A("sg"), A("pB", 0, UN), 0.0, ALU.is_gt, 0.5, ALU.subtract)
+        ts(A("tk"), A("pB", 0, UN), NS[r], ALU.mult, THR[r], ALU.is_gt)
 
-        def rest():
-            extra()
-            cp(A("sg"), A("pA", UN, 2 * UN))
-            ts(A("tk"), A("sg"), NS[r], ALU.mult, THR[r], ALU.is_gt)
+        def calls(n):
+            t, c = n // NC + 1, n % NC
+            lo, mid, hi = CW * c, CW * c + GS, CW * c + CW
+            out = {}
+            if t < 4:
+                out["g"] = lambda: gather(lo, mid)
+                out["G"] = lambda: gather(mid, hi)
+            if t < 1:
+                return out
+            bt = A("B%d" % t, lo, hi) if r == 1 else A("pY%d" % c, UN, UN + CW)
 
-        def sums(c):
-            mm(pT(c), A("nhalf"), ones, True, False)
-            mm(pT(c), TWp, last("mx", c), False, False)
-            mm(pT(c), TWn, last("mn", c), False, True)
+            def opening():
+                if n == 2 * NC:
+                    tt(A("stk"), A("sg"), A("tk"), ALU.mult)
+                mm(pT(c), A("nhalf"), A("ones", 0, CW), True, False)
+                mm(pT(c), A("CP%d" % t), A("sg" if t < 4 else "stk", lo, hi), False, False)
+                if t < 4:
+                    mm(pY(c), A("nhalf"), A("big", 0, CW), True, False)
+                    mm(pY(c), A("I16"), A("Xs", lo, hi), False, False)
 
-        def keep(c, t):
-            tt(cc("u", c), pT(c), cc("sg", c), ALU.mult)
-            yield
-            bt = cc("B%d" % t, c) if r == 1 else pS(c, 2)
-            ts(bt, cc("u", c), PBS[t], ALU.mult, 0.0, ALU.is_gt)
-            yield
-            if t == 4:
-                tt(pS(c, 3), bt, cc("VT", c), ALU.mult)
-                yield
-                tt(cc("Xf", c), pS(c, 3), cc("Xs", c), ALU.add)
-                return
-            tt(cc("V", c), bt, cc("V", c), ALU.mult)
-            mm(pS(c), A("L%d" % (t + 1)), cc("V", c))
-            mm(pY(c), A("I16"), cc("Xs", c), True, False)
-            mm(pY(c), A("I%d" % (t + 1)), cc("V", c), False, True)
-            yield
-            if t == 3:
-                tt(cc("VT", c), cc("tk", c), cc("V", c), ALU.mult)
-            for _ in tail(c, None):
-                yield
-            gather(c)
+            def scans(f, a, b, first=False, end=False):
+                def call():
+                    if first:
+                        opening()
+                    f(a, b)
+                    if b == hi:
+                        mm(pT(c), TWp if f is smax else TWn, last("mx" if f is smax else "mn", lo, hi), False, end)
+                return call
 
-        before = iter(())
-        for t in (1, 2, 3, 4):
-            for c in range(NC):
-                now = keep(c, t)
-                for x in STEP:
-                    if x == "p":
-                        next(before, None)
-                    elif x == "h":
-                        if rest:
-                            rest()
-                            rest = None
-                        next(now)
-                    else:
-                        (smax if x in "ab" else smin)(c, *PIECE[x])
-                        if x == "D":
-                            sums(c)
-                run(before)
-                before = now
-        if r == 1:
-            for t in (1, 2, 3, 4):
-                mm(A("pA", 0, UN), A("AW%d" % t), A("B%d" % t), t == 1, t == 4)
-        run(before)
+            def d():
+                ts(bt, pT(c), BAND, ALU.add, BAND, ALU.not_equal)
+                if t < 4:
+                    mm(pS(c), A("L"), A("Xs", lo, hi), True, False)
+                    mm(A("pB", 0, CW), A("L"), A("Xs", lo, hi), True, False)
+                if r == 1 and t == 4:
+                    mm(A("pA", lo, hi), A("AW4"), bt, False, c == NC - 1)
+                if r == 1 and t < 4 and c == NC - 1:
+                    mm(A("pA", 0, UN), A("AW%d" % t), A("B%d" % t), t == 1, False)
 
-    landed("ad", 3 * neng, [("RD", 3 * a + c) for a in peers for c in range(3)])
-    iota_row(0, UN)
+            def e():
+                tt(A("V", lo, hi), bt, A("V", lo, hi), ALU.mult)
+                if t < 4:
+                    mm(pS(c), A("L%d" % (t + 1)), A("V", lo, hi), False, True)
+                    mm(A("pB", 0, CW), A("L%d" % (t + 1)), A("V", lo, hi), False, False)
+                    mm(pY(c), A("I%d" % (t + 1)), A("V", lo, hi), False, True)
+            out.update({"A": scans(smax, lo, hi, True), "B": scans(smin, lo, hi, False, True),
+                        "a": scans(smax, lo, mid, True), "b": scans(smin, lo, mid),
+                        "x": scans(smax, mid, hi), "y": scans(smin, mid, hi, False, True), "d": d, "e": e})
+            if t < 4:
+                out.update(tail(c, A("pB", 0, CW), lo, hi, lift))
+            return out
+
+        chunks = {n: calls(n) for n in range(-NC, 4 * NC)}
+        for n in range(-NC, 4 * NC + 2):
+            for x in SLOT.split():
+                call = chunks.get(n - int(x[1]), {}).get(x[0])
+                if call:
+                    call()
+
+    landed("ad", 3 * neng, [("RD", 12 * a + c) for a in peers for c in range(12)])
+    for bank in ("pA", "pB"):
+        iota_row(bank)
     for n, a in enumerate([j] + peers):
-        z = A("ZL" if a % 2 == 0 else "ZH", 96 - 32 * a, 224 - 32 * a)
-        mm(A("pA", 0, UN), z, A("RD", UN * a, UN * a + UN), False, n == 3)
+        for bank in ("pA", "pB"):
+            z = A("ZL" if a % 2 == 0 else "ZH", 96 - 32 * a, 224 - 32 * a)
+            mm(A(bank, 0, UN), z, A("RD", UN * a, UN * a + UN), False, n == 3)
     sort("R1")
-    search(1, "R1", 0.0, lambda: None)
-    cp(A("Xq"), ind(A("Xf"), A("R1")))
-    emit("v", lambda: g.vector.tensor_reduce(out=T.Acol[:, :], in_=A("pA", 0, UN)[0], axis=AxisListType.X, op=ALU.add),
-         [A("pA", 0, UN)], [A("Acol")])
+    search(1, "R1", Xq, lift1, lambda: None)
+    tt(A("Xn"), ind(A("V"), A("R1")), Xq, ALU.add)
+    act(A("KM"), A("pA", 0, UN), ACT.Copy, acc=A("Acol", 0, 1))
+    act(A("Acol", 1, 2), A("Acol", 0, 1), ACT.Identity, bias=LC)
+    ts(A("Acol", 2, 3), A("Acol", 0, 1), LIFT - 2047.5, ALU.add)
+    lift2 = (A("Acol", 2, 3), A("Acol", 1, 2))
 
-    def keys2(c):
-        lo, hi = CW * c, CW * c + CW
-        iota_row(lo, hi)
-        mm(A("pA", lo, hi), A("KWp"), last("mx", c), False, False)
-        mm(A("pA", lo, hi), A("KWn"), last("mn", c), False, True)
+    columns(A("L"), A("I16"), "Xn", M2_S[0], lift2)
+    for bank in ("pA", "pB"):
+        iota_row(bank)
+    done = [0]
 
-    for _ in measure("Xq", A("Acol"), keys2):
-        pass
+    def keys2(lo, hi):
+        done[0] += hi - lo
+        for bank in ("pA", "pB"):
+            mm(A(bank, lo, hi), A("KWp"), last("mx", lo, hi), False, False)
+            mm(A(bank, lo, hi), A("KWn"), last("mn", lo, hi), False, done[0] == UN)
+
+    measure(M2_S, M2_V, keys2)
+    mm(A("pY2", 0, UN), A("KWp"), last("mx", 0, UN), True, False)
+    mm(A("pY2", 0, UN), A("KWn"), last("mn", 0, UN), False, True)
     sort("R2")
-    for c in range(NC):
-        q_ = A("pB", UN + CW * c, UN + CW * c + CW)
-        mm(q_, A("QWp"), last("mx", c), True, False)
-        mm(q_, A("QWn"), last("mn", c), False, True)
-
-    def send_q():
-        cp(A("qs"), A("pB", UN, 2 * UN))
-        fan(A("qs"), "lq", "aq")
-
-    search(2, "R2", A("Acol"), send_q)
+    act(A("qs"), A("pY2", 0, UN), ACT.Copy, scale=QS)
+    fan(A("qs"), "lq", "aq")
+    search(2, "R2", A("Xn"), lift2, lambda: None)
 
     landed("aq", 3 * neng, [("lq", a) for a in peers])
     for a in [j] + peers:
@@ -560,7 +584,7 @@ def rank_program(g, core, T, topo):
         name = "qs" if a == j else "lq"
         src = A(name, lo, lo + UN)
         dma("y", T.yq[2 * a:2 * a + 2, :], T[name][32 * j:32 * j + 32:16, lo:lo + UN], [src])
-    ts(A("yo"), ind(A("Xf"), A("R2")), BIG, ALU.add)
+    tt(A("yo"), ind(A("V"), A("R2")), A("Xn"), ALU.add)
     fan(A("yo"), "ly", "ay")
     landed("ay", 3 * neng, [("ly", a) for a in peers])
     for n, a in enumerate([j] + peers):

@@ -9,11 +9,31 @@ CW = 64
 GS = 32
 LIFT = 160 * 4096.0
 BAND = 1.5 * 2.0 ** 36
-SLOT = "A0 g2 r1 B0 q1 G2 d0 f1 e0 h1 k1"
-M1_S, M1_V = (64, 64, 32, 16), 16
-M2_S, M2_V = (32, 64, 64, 16), 16
+SLOT = "a0 f2 G3 d1 h2 e1 k2 b0 x0 r1 o0 y0 g2 q1"
+COLUMNS = {False: "S0 r0 S1 Z1 m0 Y0 r1 q0 f0 Y1 q1 h0 k0 f1 g0 h1 k1",
+           "r1": "K0 S0 S1 Y0 r0 m0 Z1 r1 q0 q1 f0 Y1 h0 k0 W0 g0 s0 t0 f1 h1 v0 k1 p0",
+           "r2": "K0 S0 S1 W0 Y0 r0 s0 m0 Z1 r1 t0 q1 q0 f0 Y1 h0 k0 g0 f1 h1 v0 k1",
+           True: "S0 S1 Z0 r0 Z1 Y0 r1 q0 f0 Y1 k0 q1 g0 f1 v0 k1"}
+MOD, CMOD = "T", "VT"
+SHARE = (0, 0, 0)
+FIRST_V = 0
+JOIN = 1
+ZB = ("pB", "pB")
+GL = 32
+RS = (0, 1, 2)
+VCOPY = "v"
+LAST = {1: "G3 a0 d1 b0 e1 x0 y0"}
+CUT = 64
+M1_S, M1_V = (64, 48, 32, 16), 32
+M2_S, M2_V = (32, 32, 48, 32, 16), 32
+LAST_V = (0, 0, 0)
+WIDE = 5
 SORT_S = 7
-EARLY = 6144
+EARLY = 64
+AHEAD, LOADS = 2, 0
+W = 8192
+KEY = 2.0 ** 22
+WHOLE = 1.5 * 2.0 ** 23
 
 SCRATCH = {}
 GRAN = {}
@@ -26,14 +46,14 @@ def _buf(names, cols, dtype, gran=None, where="sbuf"):
 
 
 _buf("U32", UN, "int32")
-_buf("lu", 4 * UN, "float32", UN)
-_buf("shelfs", 8192, "bfloat16", 2048)
-_buf("Xo Xq Xn Xs V ks kss yo qs w2", UN, "float32", 16)
-_buf("ci cj", UN, "int32", 16)
-_buf("off", UN, "uint16", 16)
-_buf("gv mx mn", UN * 16, "bfloat16", 256)
-_buf("B1 B2 B3 B4 rq sg tk stk", UN, "bfloat16", 16)
-_buf("RD", 4 * UN, "bfloat16", 16)
+_buf("Uq", UN, "int32")
+_buf("shelfs", 2 * W, "bfloat16", 2048)
+_buf("Xo Xq Xn Xs V ks kss yo qs w2", UN, "float32", 8)
+_buf("ci cj", UN, "int32", 8)
+_buf("off", UN, "uint16", 8)
+_buf("gv mx mn", UN * 16, "bfloat16", 128)
+_buf("B1 B2 B3 B4 rq rw sg tk stk", UN, "bfloat16", 8)
+_buf("RD", 4 * UN, "bfloat16", 8)
 _buf("lq ly", 4 * UN, "float32", UN)
 _buf("KM Kc", UN, "float32")
 _buf("cmp", 6 * UN, "bfloat16", UN)
@@ -41,31 +61,33 @@ _buf("cmps", 6 * UN, "bfloat16")
 _buf("sj", 12 * UN, "bfloat16", UN)
 _buf("acc", 16, "float32", 1)
 _buf("R1 R2", 12, "uint16", 1)
-_buf("Acol", 4, "float32", 1)
-_buf("mmax mmin", CW * 16, "bfloat16")
+_buf("Acol", 8, "float32", 1)
+_buf("mmax mmin", 1024, "bfloat16")
 _buf("rkm", 6 * UN, "bfloat16")
-_buf("m16 diag uf", UN, "float32")
-_buf("it on1 big", UN, "bfloat16")
-_buf("ones", 6 * UN, "bfloat16")
-_buf("nhalf RM", 128, "bfloat16")
-_buf("mm mi mG mP1 mP2", 128, "float32", 64)
+_buf("m16 diag uf uu", UN, "float32")
+_buf("it big half neg", UN, "bfloat16")
+_buf("ones", 96, "bfloat16")
+_buf("nhalf RM RW", 128, "bfloat16")
+_buf("mG mP1 mP2", 128, "float32")
 _buf("ic", 24, "int32", 1)
 _buf("fc", 96, "float32", 1)
-_buf("SG TR L NEQ I16", 128, "float32")
+_buf("SG TR L NEQ I16 EQ E16", 128, "float32")
 for _r in "12":
     for _n in ("M0", "M1", "Y1", "DP", "SW", "PG"):
         _buf(_n + _r, 128, "float32")
     _buf("TWp%s TWn%s" % (_r, _r), 128, "bfloat16")
-_buf("L2 L3 L4 I2 I3 I4", 128, "float32")
+_buf("L2 L3 L4 I2 I3 I4 J2 J3 J4", 128, "float32")
 _buf("AW1 AW2 AW3 AW4 CP1 CP2 CP3 CP4 KWp KWn", 128, "bfloat16")
 _buf("ZL ZH", 224, "bfloat16")
 _buf("pS0 pS1 pS2 pY0 pY1 pY2 pA pB", 512, "float32", None, "psum")
 PSUM = {n for n in SCRATCH if SCRATCH[n][0] == "psum"}
 SCRATCH["st"] = ("dram", [4, 128, 2048], "bfloat16")
 SCRATCH["rv"] = ("dram", [4, 128, 2048], "bfloat16")
+SCRATCH["su"] = ("dram", [4, 128, UN // 4], "int32")
+SCRATCH["ru"] = ("dram", [4, 128, UN // 4], "int32")
 
-NDMA = 24
-SEMAPHORES = (["cv", "cs", "ct", "cg", "lo", "lr", "au", "ad", "aq", "ay"] + ["as%d" % a for a in range(4)]
+NDMA = 28
+SEMAPHORES = (["cv", "cs", "ct", "cg", "lo", "lr", "au", "aq"] + [n % a for n in ("as%d", "ad%d", "ay%d") for a in range(4)]
               + ["d%d" % k for k in range(NDMA)])
 
 
@@ -227,85 +249,161 @@ def rank_program(g, core, T, topo):
     def fc(k):
         return A("fc", k, k + 1)
 
+    def send(src, dst, sem, some):
+        engines = topo.engines(core, quad[some[0]])
+        part = 1 << ((len(engines) // len(some)).bit_length() - 1)
+        transfers = []
+        for n, a in enumerate(some):
+            rid, pid, _ = topo.addr(quad[a])
+            transfers.append(RemoteDMATransfer(dst_ids=[DstId(rid=rid, pnc=pid)], remote_sem=T.sem[sem], src=src[a], dst=dst[j],
+                                               dma_engine_mask=sum(1 << e for e in engines[part * n:part * n + part])))
+        g.remote_dma_fused(transfers, local_sem=T.sem.lo)
+        count["lo"] = count.get("lo", 0) + part * len(some)
+        return part
+
+    staged = dma("s", T.su[:, :, :], T.units[:, :])
     dma("y", T.U32[:, :], T.units[:, :], [], [A("U32")])
-    early = dma("y", T.shelfs[:, :EARLY], T.shelf[:, :EARLY], [], [A("shelfs", 0, EARLY)])
-    dma("y", T.shelfs[:, EARLY:], T.shelf[:, EARLY:], [], [A("shelfs", EARLY)])
+    early = dma("y", T.shelfs[:EARLY, :W], T.shelf[:EARLY, :], [], [(None, [("early", 0)])])
+    dma("y", T.shelfs[EARLY:, :W], T.shelf[EARLY:, :], [], [A("shelfs", 0, W)])
+    window = [W, [early]]
     need("y", early)
     stage = {}
     for a in peers:
         stage[a] = dma("y", T.st[a], T.shelf[32 * a:32 * a + 32, :])
 
     iota(ic(0), [[0, 1]], 0, 1)
-    iota(A("mi"), [[0, 8], [1, 16]])
+    iota(A("uu"), [[1, UN]])
+    iota(A("uf"), [[0, 12], [1, 16]])
     iota(A("mG"), [[1, 8], [0, 16]])
-    iota(A("mm"), [[1, 128]])
-    fill(A("ones"), 1.0)
+    need("g", staged)
+    came = send(T.su, T.ru, "au", peers)
+    mm_, mi = A("uu", 0, 128), A("uf", 0, 128)
     fill(A("nhalf"), -1.0 / 256)
-    fill(A("big"), 2.0 ** 24)
     ts(ic(1), ic(0), 15, ALU.bitwise_and)
     ts(ic(2), ic(0), 4, ALU.logical_shift_right)
     for k in range(7):
         ts(ic(3 + k), ic(0), k, ALU.logical_shift_right, 1, ALU.bitwise_and)
+    fill(A("ones"), 1.0)
     cp(A("fc", 0, 10), A("ic", 0, 10))
+    fill(A("big"), 2.0 ** 24)
     P_, PI, PG_ = fc(0), fc(1), fc(2)
-    ts(A("TR"), A("mi"), PI, ALU.is_ge)
-    cp(A("Xo"), A("U32"))
-    ts(A("SG"), A("mG"), PG_, ALU.is_equal)
-    ts(A("NEQ"), A("mm"), P_, ALU.is_equal, -1.0, ALU.mult)
-    tt(A("L"), A("SG"), A("TR"), ALU.mult)
-    fan(A("Xo"), "lu", "au")
-    act(A("I16"), A("NEQ"), ACT.Copy, scale=-16.0)
-    act(A("RM"), A("NEQ"), ACT.Copy, scale=4096.0)
+    ts(A("NEQ"), mm_, P_, ALU.is_equal, -1.0, ALU.mult)
 
-    def pS(c, n=CW):
-        return A("pS%d" % c, 0, n)
+    def bits(base):
+        return A("fc", base, base + 7)
+    ts(bits(10), bits(3), -1.0, ALU.mult, 1.0, ALU.add)
+    ts(bits(17), bits(3), -2.0, ALU.mult, 1.0, ALU.add)
+    ts(bits(24), bits(3), 2.0, ALU.mult, -1.0, ALU.add)
+    ts(bits(31), bits(3), 16.0, ALU.mult, -16.0, ALU.add)
+    ts(bits(82), bits(3), 1.0, ALU.mult, -1.0, ALU.add)
+    ts(bits(59), bits(3), -8192.0, ALU.mult, 4096.0, ALU.add)
+    ts(fc(59), fc(3), -4096.0, ALU.mult, 2048.0, ALU.add)
+    ts(A("TR"), mi, PI, ALU.is_ge)
+    ts(A("SG"), A("mG"), PG_, ALU.is_equal)
+    cp(A("Xo"), A("U32"))
+    tt(A("L"), A("SG"), A("TR"), ALU.mult)
+    ts(bits(38), bits(24), 448.0 + 2 * KEY, ALU.mult)
+    ts(bits(45), bits(17), 512.0, ALU.mult)
+    ts(bits(52), bits(24), 512.0, ALU.mult)
+    LOWC, L16, L1, PB = ({t: fc(b + 4 - t) for t in (1, 2, 3, 4)} for b in (10, 31, 82, 59))
+    SIDE, NS, THR = ({r: fc(b + 4 + r) for r in (1, 2)} for b in (17, 24, 38))
+    K512, K512N = fc(52 + 6), fc(45 + 6)
+
+    def scaled(out, a, col):
+        act(A(out), A(a), ACT.Copy, scale=col)
+
+    for name, x in (("I16", -16.0), ("RM", 4096.0), ("EQ", -1.0), ("E16", -1.0 / 16), ("RW", 8192.0))[:5 if WIDE < 5 else 2]:
+        scaled(name, "NEQ", x)
+    for t in (1, 2, 3, 4):
+        scaled("CP%d" % t, "NEQ", PB[t])
+
+    def pS(c, n=None):
+        return A("pS%d" % c, 0, n or CW)
 
     def pT(c):
         return A("pS%d" % c, UN, UN + CW)
 
-    def pY(c, n=CW):
-        return A("pY%d" % c, 0, n)
+    def pY(c, n=None):
+        return A("pY%d" % c, 0, n or CW)
 
-    def tail(c, z, lo, hi, lift):
+    def tail(c, z, lo, hi, lift, wide, by="v"):
+        y = pY(c, hi - lo)
+
         def r():
-            ts(A("rq", lo, hi), pS(c, hi - lo), lift[0], ALU.add, 2.0 ** -12, ALU.mult)
+            if by == "s":
+                act(A("rq", lo, hi), pS(c, hi - lo), ACT.Identity, bias=lift[2], scale=2.0 ** -12)
+            else:
+                ts(A("rq", lo, hi), pS(c, hi - lo), lift[0], ALU.add, 2.0 ** -12, ALU.mult)
             mm(z, A("RM"), A("rq", lo, hi), False, True)
-        return {"r": r,
-                "q": lambda: act(A("w2", lo, hi), z, ACT.Square, bias=lift[1]),
-                "f": lambda: tt(A("ci", lo, hi), A("w2", lo, hi), pY(c, hi - lo), ALU.add),
-                "h": lambda: ts(A("cj", lo, hi), A("ci", lo, hi), 4, ALU.arith_shift_right, 8191, ALU.bitwise_and),
-                "k": lambda: cp(A("off", lo, hi), A("cj", lo, hi))}
 
-    def columns(ls, ly, X, cut, lift, between=None):
-        parts = [(c, lo, hi) for c, (lo, hi) in enumerate(((0, cut), (cut, UN))) if hi > lo]
-        for c, lo, hi in parts:
-            mm(pY(c, hi - lo), A("nhalf"), A("big", lo, hi), True, False)
-        for c, lo, hi in parts:
-            mm(pS(c, hi - lo), ls, A(X, lo, hi))
-            mm((pS, pY)[c](2, hi - lo), ls, A(X, lo, hi), True, False)
-        for c, lo, hi in parts:
-            mm(pY(c, hi - lo), ly, A(X, lo, hi), False, True)
-        calls = [tail(c, (pS, pY)[c](2, hi - lo), lo, hi, lift) for c, lo, hi in parts]
-        for x in "rq":
-            for t in calls:
-                t[x]()
-        if between:
-            between()
-        for t in calls:
-            for x in "fhk":
-                t[x]()
+        def q():
+            act(A("w2", lo, hi), z, ACT.Square, bias=lift[1])
+            if wide:
+                mm(y, A("E16"), A("w2", lo, hi), False, False)
+
+        def f():
+            ts(A("rw", lo, hi), A("w2", lo, hi), 2.0 ** -17, ALU.mult, 128.5 - 2.0 ** -15, ALU.add)
+            mm(y, A("RW"), A("rw", lo, hi), False, True)
+        def square():
+            tt(A("w2", lo, hi), A("cj", lo, hi), A("cj", lo, hi), ALU.mult)
+            if wide:
+                mm(y, A("E16"), A("w2", lo, hi), False, False)
+        if z is None:
+            out = {"r": lambda: ts(A("ci", lo, hi), pS(c, hi - lo), lift[1], ALU.add),
+                   "m": lambda: ts(A("cj", lo, hi), A("ci", lo, hi), 4095, ALU.bitwise_and), "q": square}
+        else:
+            out = {"r": r, "q": q}
+        if wide:
+            out.update({"f": f, "k": lambda: ts(A("off", lo, hi), y, WHOLE + 129 * W, ALU.add, WHOLE, ALU.subtract)})
+        else:
+            out.update({"f": lambda: tt(A("ci", lo, hi), A("w2", lo, hi), y, ALU.add),
+                        "h": lambda: ts(A("cj", lo, hi), A("ci", lo, hi), 4, ALU.arith_shift_right, W - 1, ALU.bitwise_and),
+                        "k": lambda: cp(A("off", lo, hi), A("cj", lo, hi))})
+        return out
+
+    def opened(c, lo, hi, wide):
+        mm(pY(c, hi - lo), A("nhalf"), A("half" if wide else "big", lo, hi), True, False)
+
+    def columns(ls, ly, X, cut, lift, wide, suspects=None, order=None):
+        parts = []
+        for c, (lo, hi) in enumerate(((0, cut), (cut, UN))):
+            if hi == lo:
+                parts.append({})
+                continue
+            opened(c, lo, hi, wide)
+            z = (pS, pY)[c](2, hi - lo) if CMOD[c] != "V" else None
+            calls = tail(c, z, lo, hi, lift, wide, "s" if CMOD[c] == "S" else "v")
+            calls["S"] = lambda c=c, lo=lo, hi=hi: mm(pS(c, hi - lo), ls, A(X, lo, hi))
+            if z:
+                calls["Z"] = lambda z=z, lo=lo, hi=hi: mm(z, ls, A(X, lo, hi), True, False)
+            calls["Y"] = lambda c=c, lo=lo, hi=hi: mm(pY(c, hi - lo), ly, A(X, lo, hi), False, not wide)
+            parts.append(calls)
+        parts[0].update(suspects or {})
+        if cut < UN:
+            parts[0]["g"] = lambda: gather(0, GS)
+        for x in (order or COLUMNS[wide]).split():
+            call = parts[int(x[1])].get(x[0])
+            if call:
+                call()
 
     def ew(name, lo, hi):
         return A(name, 16 * lo, 16 * hi)
 
-    def picks(lo, hi):
-        return ind(A("shelfs"), A("off", lo, hi))
+    def picks(q, lo, hi):
+        for tok in window[1]:
+            need(q, tok)
+        return ind(A("shelfs", 0, window[0]), A("off", lo, hi))
 
     def gather(lo, hi):
-        act(ew("gv", lo, hi), picks(lo, hi), ACT.Copy)
+        if hi > lo:
+            act(ew("gv", lo, hi), picks("s", lo, hi), ACT.Copy)
+
+    def vgather(lo, hi):
+        if hi > lo:
+            cp(ew("gv", lo, hi), picks("v", lo, hi))
 
     def smax(lo, hi):
-        scan(ew("mx", lo, hi), A("mmax", 0, 16 * (hi - lo)), ew("gv", lo, hi), 0.0, ALU.mult, ALU.max)
+        scan(ew("mx", lo, hi), A("mmax", 0, 16 * (hi - lo)), ew("gv", lo, hi), 0.0, ALU.min, ALU.max)
 
     def smin(lo, hi):
         scan(ew("mn", lo, hi), A("mmin", 0, 16 * (hi - lo)), ew("gv", lo, hi), 0.0, ALU.add, ALU.min)
@@ -313,13 +411,15 @@ def rank_program(g, core, T, topo):
     def last(name, lo, hi):
         return A(name, 16 * lo + 15, 16 * hi, 16)
 
-    def measure(pieces, own, after):
+    def measure(pieces, own, after, begun=0):
         cuts = [sum(pieces[:k]) for k in range(len(pieces) + 1)]
-        for lo, hi in zip(cuts, cuts[1:]):
+        for lo, hi in zip(cuts[begun:], cuts[begun + 1:]):
             gather(lo, hi)
+        if begun and JOIN:
+            del cuts[1]
         order = list(zip(cuts, cuts[1:]))
         if own:
-            cp(ew("gv", UN - own, UN), picks(UN - own, UN))
+            vgather(UN - own, UN)
             order = [(UN - own, UN)] + order
         for lo, hi in order:
             smax(lo, hi)
@@ -328,36 +428,15 @@ def rank_program(g, core, T, topo):
 
     LC = fc(90)
     fill(LC, LIFT)
-    lift1 = (LIFT - 2047.5, LC)
-    columns(A("L"), A("I16"), "Xo", UN, lift1)
-
-    def mask_fill(name, one, at, step, n):
-        fill(A(name), one)
-        fill(A(name, 0, n, step), at)
-
-    mask_fill("mmax", 1.0, 0.0, 16, 16 * CW)
-    mask_fill("mmin", 0.0, 512.0, 16, 16 * CW)
-
-    iota(A("uf"), [[0, 12], [1, 16]])
-    iota(A("it"), [[-2, UN]], -2)
-    for h in (0, 1):
-        iota(A("mP1", 64 * h, 64 * h + 64), [[0, 2], [1, 2], [0, 16]], 4 * h)
-    iota(A("mP2"), [[0, 2], [1, 4], [0, 16]])
-    select(A("DP1"), A("NEQ"), [[-64, 2], [32, 2], [-1, 32]], ALU.not_equal, 1.0, -32, 1)
-
-    def bits(base):
-        return A("fc", base, base + 7)
-    ts(bits(10), bits(3), -1.0, ALU.mult, 1.0, ALU.add)
-    ts(bits(17), bits(3), -2.0, ALU.mult, 1.0, ALU.add)
-    ts(bits(24), bits(3), 2.0, ALU.mult, -1.0, ALU.add)
-    ts(bits(31), bits(10), -16.0, ALU.mult)
-    ts(bits(38), bits(17), 448.0, ALU.mult)
-    ts(bits(45), bits(17), 512.0, ALU.mult)
-    ts(bits(52), bits(24), 512.0, ALU.mult)
-    ts(bits(59), bits(17), 8192.0, ALU.mult)
-    LOWC, L16, PB = ({t: fc(b + 4 - t) for t in (1, 2, 3, 4)} for b in (10, 31, 59))
-    SIDE, NS, THR = ({r: fc(b + 4 + r) for r in (1, 2)} for b in (17, 24, 38))
-    K512, K512N = fc(52 + 6), fc(45 + 6)
+    fill(fc(95), (LIFT - 2047.5) / 4096)
+    lift1 = (LIFT - 2047.5, LC, fc(95))
+    fill(A("mmin"), 0.0)
+    fill(fc(91), 512.0)
+    fill(fc(92), -2.0)
+    fill(A("mmin", 0, 1024, 16), 512.0)
+    columns(A("L"), A("I16"), "Xo", UN, lift1, False)
+    act(A("mmax"), A("mmin"), ACT.Identity, bias=fc(91), scale=-1.0)
+    act(A("it"), A("uu"), ACT.Identity, bias=fc(92), scale=-2.0)
     Z0, Z15, Z15L, GB, QS = fc(66), fc(67), fc(68), fc(69), fc(70)
     ts(Z0, PI, 0.0, ALU.is_equal, -1.0, ALU.mult)
     ts(Z15, PI, 15.0, ALU.is_equal)
@@ -367,19 +446,18 @@ def rank_program(g, core, T, topo):
     SRC, GRP, PAIR = {}, {}, {}
     for r, X in ((1, 32.0), (2, 64.0)):
         SRC[r], GRP[r], PAIR[r] = fc(71 + r), fc(74 + r), fc(77 + r)
-        ts(fc(80 + r), SIDE[r], LOWC[1], ALU.mult)
-        ts(PAIR[r], fc(7 + r), -X / 16, ALU.mult, PG_, ALU.add)
+        ts(fc(92 + r), SIDE[r], LOWC[1], ALU.mult)
+        ts(PAIR[r], NS[r], X / 32, ALU.mult, PG_, ALU.subtract)
     for r, X in ((1, 32.0), (2, 64.0)):
-        ts(SRC[r], fc(80 + r), X, ALU.mult, P_, ALU.add)
-        ts(GRP[r], fc(80 + r), X / 16, ALU.mult, PG_, ALU.add)
+        ts(SRC[r], fc(92 + r), X, ALU.mult, P_, ALU.add)
+        ts(GRP[r], fc(92 + r), X / 16, ALU.mult, PG_, ALU.add)
 
-    def scaled(out, a, col):
-        act(A(out), A(a), ACT.Copy, scale=col)
-
-    def pair_matrices(r):
+    def pair_groups(r):
+        ts(A("PG%d" % r), A("mP%d" % r), float(r), ALU.is_equal)
         ts(A("M0%d" % r), A("mG"), GRP[r], ALU.is_equal)
-        ts(A("PG%d" % r), A("mP%d" % r), PAIR[r], ALU.is_equal)
-        ts(A("Y1%d" % r), A("mm"), SRC[r], ALU.is_equal, 16.0, ALU.mult)
+
+    def pair_sums(r):
+        ts(A("Y1%d" % r), mm_, SRC[r], ALU.is_equal, 1.0 if r == 2 and WIDE < 5 else 16.0, ALU.mult)
         tt(A("M1%d" % r), A("M0%d" % r), A("TR"), ALU.mult)
 
     def pair_scaled(r):
@@ -387,25 +465,20 @@ def rank_program(g, core, T, topo):
         scaled("TWn%d" % r, "PG%d" % r, NS[r])
         scaled("SW%d" % r, "PG%d" % r, Z0)
 
-    for t in (2, 3, 4):
-        scaled("L%d" % t, "L", LOWC[t])
-        scaled("I%d" % t, "NEQ", L16[t])
-    for t in (1, 2, 3, 4):
-        scaled("CP%d" % t, "NEQ", PB[t])
-    scaled("KWp", "SG", K512)
-    scaled("KWn", "SG", K512N)
     fill(A("ZL"), 0.0)
+    fill(A("neg"), -2 * KEY)
     ts(A("diag"), A("uf"), PI, ALU.is_equal)
     ts(A("ZL", 96, 128), A("mG", 0, 32), GB, ALU.is_equal, -512.0, ALU.mult)
-    ts(A("m16"), A("uf"), 0.0, ALU.is_gt)
-    pair_matrices(1)
-    act(A("ZH"), A("ZL"), ACT.Copy, scale=-1.0)
+    for r in (1, 2):
+        act(A("mP%d" % r), A("mG"), ACT.Abs, bias=PAIR[r])
 
-    def pass_on(a):
-        need("g", stage[a])
-        rid, pid, _ = topo.addr(quad[a])
-        g.remote_dma(T.rv[j], T.st[a], T.sem["as%d" % j], T.sem.lo, pid, rid, topo.mask(core, quad[a]))
-        count["lo"] += neng
+    share = {}
+
+    def pass_on(some):
+        for a in some:
+            need("g", stage[a])
+        part = send(T.st, T.rv, "as%d" % j, some)
+        share.update({a: part for a in some})
 
     def ranges(lo, hi):
         tt(A("RD", UN * j + lo, UN * j + hi), last("mx", lo, hi), last("mn", lo, hi), ALU.subtract)
@@ -419,38 +492,60 @@ def rank_program(g, core, T, topo):
         if hi == UN - M1_V:
             ranges(lo, UN)
 
-    pass_on(peers[0])
-    select(A("rkm", 0, (12 - SORT_S) * UN), A("ones", 0, (12 - SORT_S) * UN), [[0, 12 - SORT_S], [1, UN]], ALU.is_gt, 0.0)
-    pass_on(peers[1])
+    for a in peers[:AHEAD]:
+        pass_on([a])
     measure(M1_S, M1_V, ranges_late)
-    fan(A("RD", UN * j, UN * j + UN), "RD", "ad", "lr")
-    pass_on(peers[2])
+    fan(A("RD", UN * j, UN * j + UN), "RD", "ad%d" % j)
+    g.sem_inc(T.sem.lr, 1)
+    count["lr"] = 1
+    if AHEAD < 3:
+        pass_on(peers[AHEAD:])
+    select(A("DP1"), A("NEQ"), [[-64, 2], [32, 2], [-1, 32]], ALU.not_equal, 1.0, -32, 1)
     select(A("DP2"), A("NEQ"), [[64, 2], [-1, 64]], ALU.not_equal, 1.0, -64, 1)
 
-    pair_matrices(2)
+    act(A("ZH"), A("ZL"), ACT.Copy, scale=-1.0)
+    fill(A("rkm", 0, (12 - SORT_S) * UN), 256.0)
+    ts(A("m16"), A("uf"), 0.0, ALU.is_gt)
+    LARGER = fc(89)
+    fill(LARGER, 2 * KEY - 63)
+    fill(A("rkm", 0, (12 - SORT_S) * UN, UN), 0.0)
+    pair_groups(1)
+    pair_sums(1)
+    if WIDE < 5:
+        fill(A("half"), 0.5)
+    for t in (2, 3, 4):
+        scaled("L%d" % t, "L", LOWC[t])
+        if WIDE < 5:
+            scaled("J%d" % t, "NEQ", L1[t])
+    for t in range(2, min(WIDE, 4) + 1):
+        scaled("I%d" % t, "NEQ", L16[t])
     pair_scaled(1)
     scaled("AW1", "PG1", Z15L)
     scaled("AW4", "PG1", Z15)
     for t in (2, 3):
         act(A("AW%d" % t), A("AW1"), ACT.Copy, scale=2.0 ** (1 - t))
-    pair_scaled(2)
 
-    landed("au", 3 * neng, [("lu", a) for a in peers])
-    for a in range(4):
-        src = A("Xo", 0, UN, None, 32 * j, 32 * j + 32) if a == j else A("lu", UN * a, UN * a + UN, None, 32 * j, 32 * j + 32)
-        dma("y", T.Xq[32 * a:32 * a + 32, :], src[0], [src], [(None, [("Xq4", a)])])
-    Xq = (T.Xq[:, :], [("Xq4", a) for a in range(4)])
-    own_reads = list(state[("shelfs", 0)]["r"].values())
-    loads = []
-    need("y", ("lr", neng, None, {}))
+    landed("au", 3 * came, [("ru", 0)])
+    dma("y", T.Uq[32 * j:32 * j + 32, :], T.units[32 * j:32 * j + 32, :], [], [(None, [("Uq4", j)])])
     for a in peers:
-        landed("as%d" % a, neng, [("rv", a)])
+        dma("y", T.Uq[32 * a:32 * a + 32, :], T.ru[a], [(None, [("ru", 0)])], [(None, [("Uq4", a)])])
+    own_reads = list(state[("shelfs", 0)]["r"].values())
+    for n, a in enumerate(peers):
+        if n == LOADS:
+            need("y", ("lr", 1, None, {}))
+        landed("as%d" % a, share[a], [("rv", a)])
         for t in own_reads:
             need("y", t)
-        loads.append(dma("y", T.shelfs[32 * a:32 * a + 32, :], T.rv[a], [(None, [("rv", a)])], []))
+        window[1].append(dma("y", T.shelfs[32 * a:32 * a + 32, :W], T.rv[a], [(None, [("rv", a)])], []))
+    second = []
+    if WIDE < 5:
+        second.append(dma("y", T.shelfs[32 * j:32 * j + 32, W:], T.shelf[32 * j:32 * j + 32, :]))
+        for a in peers:
+            second.append(dma("y", T.shelfs[32 * a:32 * a + 32, W:], T.rv[a], [(None, [("rv", a)])], []))
 
     def iota_row(bank):
-        mm(A(bank, 0, UN), A("nhalf"), A("it"), True, False)
+        mm(A(bank, 0, UN), A("nhalf"), A("neg"), True, False)
+        mm(A(bank, 0, UN), A("nhalf"), A("it"), False, False)
 
     def sort(R):
         nv = 12 - SORT_S
@@ -464,87 +559,151 @@ def rank_program(g, core, T, topo):
             act(A("sj", UN * k, UN * k + UN), A("ks"), ACT.Sign, bias=key(k), scale=-1.0, acc=A("acc", k, k + 1))
         for k in range(nv):
             ts(A("cmp", UN * k, UN * k + UN), A("ks"), key(SORT_S + k), ALU.is_lt)
-        scan(A("cmps", 0, nv * UN), A("rkm", 0, nv * UN), A("cmp", 0, nv * UN), 0.0, ALU.mult, ALU.add)
+        if R == "R1":
+            cp(A("Xq"), (T.Uq[:, :], [("Uq4", a) for a in range(4)]))
+        scan(A("cmps", 0, nv * UN), A("rkm", 0, nv * UN), A("cmp", 0, nv * UN), 0.0, ALU.min, ALU.add)
         cp(A(R, SORT_S, 12), A("cmps", UN - 1, nv * UN, UN))
         ts(A(R, 0, SORT_S), A("acc", 0, SORT_S), 0.5, ALU.mult, 95.5, ALU.add)
 
-    def search(r, R, X, lift, extra):
+    def search(r, R, X, lift):
         TWp, TWn = A("TWp%d" % r), A("TWn%d" % r)
         scatter(A("Xs"), A(R), X)
+        if r == 1:
+            pair_groups(2)
+            late = lambda: pair_sums(2)
+        else:
+            late = None
 
         def suspects():
             mm(A("pA", 0, UN), A("DP%d" % r), A("Xs"))
-            act(A("V"), A("pA", 0, UN), ACT.Copy)
-        columns(A("M1%d" % r), A("Y1%d" % r), "Xs", CW, lift, suspects)
-        if r == 1:
-            for tok in loads:
-                need("s", tok)
-        scatter(A("kss"), A(R), A("ks"))
-        mm(A("pB", 0, UN), A("SW%d" % r), A("kss"))
-        extra()
-        ts(A("sg"), A("pB", 0, UN), 0.0, ALU.is_gt, 0.5, ALU.subtract)
-        ts(A("tk"), A("pB", 0, UN), NS[r], ALU.mult, THR[r], ALU.is_gt)
+            if VCOPY == "s":
+                act(A("V"), A("pA", 0, UN), ACT.Copy)
+            else:
+                cp(A("V"), A("pA", 0, UN))
+        far = A("pB", 0, UN)
+        more = {"v": suspects, "p": late, "u": lambda: vgather(UN - FIRST_V, UN),
+                "K": lambda: emit("s", lambda: g.scalar.activation(out=T.kss[:, :].indirect(A(R)[0]), in_=T.ks[:, :], func=ACT.Silu),
+                                  [A("ks"), A(R)], [A("kss")]),
+                "W": lambda: mm(far, A("SW%d" % r), A("kss")),
+                "s": lambda: act(A("sg"), far, ACT.Sign, bias=LARGER),
+                "t": lambda: act(A("tk"), far, ACT.Sign, bias=THR[r], scale=NS[r])}
+        columns(A("M1%d" % r), A("Y1%d" % r), "Xs", CUT, lift, r == 2 and WIDE < 5, more, COLUMNS.get("r%d" % r))
+        after_max = {2 * NC: lambda: tt(A("stk"), A("sg"), A("tk"), ALU.mult)}
 
         def calls(n):
             t, c = n // NC + 1, n % NC
             lo, mid, hi = CW * c, CW * c + GS, CW * c + CW
+            gmid = lo + GL if n == 3 * NC - 1 else mid
+            if n == 4 * NC - 1:
+                mid = lo + GL
+            wide = (r == 2 and WIDE < 5) or t >= WIDE
+            top = hi - (LAST_V[c] if t == 3 else SHARE[c] if t > 0 else FIRST_V if c == NC - 1 else 0)
             out = {}
+
+            def first_part():
+                if r == 1 and t == WIDE and c == 0:
+                    window[0] = 2 * W
+                    window[1].extend(second)
+                if n > -NC:
+                    gather(lo, gmid)
             if t < 4:
-                out["g"] = lambda: gather(lo, mid)
-                out["G"] = lambda: gather(mid, hi)
+                out["g"] = first_part
+                out["G"] = lambda: gather(gmid, top)
             if t < 1:
                 return out
-            bt = A("B%d" % t, lo, hi) if r == 1 else A("pY%d" % c, UN, UN + CW)
+            k = n % 3
+            z = A(ZB[n % 2], 0, CW) if MOD != "V" else None
+            bt = A("B%d" % t, lo, hi) if r == 1 else A("pY%d" % k, UN, UN + CW)
+
+            def sides():
+                for s in ("sg", "stk")[:1 + t // 4]:
+                    mm(pT(k), A("CP%d" % t), A(s, lo, hi), False, False)
 
             def opening():
-                if n == 2 * NC:
-                    tt(A("stk"), A("sg"), A("tk"), ALU.mult)
-                mm(pT(c), A("nhalf"), A("ones", 0, CW), True, False)
-                mm(pT(c), A("CP%d" % t), A("sg" if t < 4 else "stk", lo, hi), False, False)
+                mm(pT(k), A("nhalf"), A("ones", 0, CW), True, False)
+                sides()
+
+            def own():
                 if t < 4:
-                    mm(pY(c), A("nhalf"), A("big", 0, CW), True, False)
-                    mm(pY(c), A("I16"), A("Xs", lo, hi), False, False)
+                    opened(k, lo, hi, wide)
+                    mm(pY(k), A("EQ" if wide else "I16"), A("Xs", lo, hi), False, False)
+            out["o"] = own
 
             def scans(f, a, b, first=False, end=False):
                 def call():
                     if first:
                         opening()
                     f(a, b)
+                    if first and n in after_max:
+                        after_max[n]()
                     if b == hi:
-                        mm(pT(c), TWp if f is smax else TWn, last("mx" if f is smax else "mn", lo, hi), False, end)
+                        mm(pT(k), TWp if f is smax else TWn, last("mx" if f is smax else "mn", lo, hi), False, end)
+                return call
+
+            def closing(first):
+                cut = hi - LAST_V[c]
+
+                def call():
+                    if first:
+                        opening()
+                    for a, b in ((lo, mid), (cut, hi)) if first else ((mid, cut),):
+                        if b > a:
+                            smax(a, b)
+                            smin(a, b)
+                    if not first:
+                        mm(pT(k), TWp, last("mx", lo, hi), False, False)
+                        mm(pT(k), TWn, last("mn", lo, hi), False, True)
                 return call
 
             def d():
-                ts(bt, pT(c), BAND, ALU.add, BAND, ALU.not_equal)
+                if r == 1 and n == 4 * NC - 1:
+                    pair_scaled(2)
+                    scaled("KWp", "SG", K512)
+                    scaled("KWn", "SG", K512N)
+                ts(bt, pT(k), BAND, ALU.add, BAND, ALU.not_equal)
                 if t < 4:
-                    mm(pS(c), A("L"), A("Xs", lo, hi), True, False)
-                    mm(A("pB", 0, CW), A("L"), A("Xs", lo, hi), True, False)
-                if r == 1 and t == 4:
-                    mm(A("pA", lo, hi), A("AW4"), bt, False, c == NC - 1)
-                if r == 1 and t < 4 and c == NC - 1:
-                    mm(A("pA", 0, UN), A("AW%d" % t), A("B%d" % t), t == 1, False)
+                    mm(pS(k), A("L"), A("Xs", lo, hi), True, False)
+                    if z:
+                        mm(z, A("L"), A("Xs", lo, hi), True, False)
+                if r == 1 and t == 4 and c < NC - 1:
+                    mm(A("pA", lo, hi), A("AW4"), bt, False, c == NC - 2)
+                    if c == NC - 2:
+                        act(A("KM", 0, hi), A("pA", 0, hi), ACT.Copy, acc=A("Acol", 0, 1))
+                        act(A("Acol", 1, 2), A("Acol", 0, 1), ACT.Identity, bias=LC)
+                if r == 1 and t < 4 and c == NC - 2:
+                    mm(A("pA", 0, hi), A("AW%d" % t), A("B%d" % t, 0, hi), t == 1, False)
+                if r == 1 and n == 4 * NC - 2:
+                    for s in (1, 2, 3):
+                        mm(A("pB", 0, CW), A("AW%d" % s), A("B%d" % s, hi, UN), s == 1, False)
+                if r == 1 and n == 4 * NC - 1:
+                    mm(A("pB", 0, CW), A("AW4"), bt, False, True)
 
             def e():
                 tt(A("V", lo, hi), bt, A("V", lo, hi), ALU.mult)
                 if t < 4:
-                    mm(pS(c), A("L%d" % (t + 1)), A("V", lo, hi), False, True)
-                    mm(A("pB", 0, CW), A("L%d" % (t + 1)), A("V", lo, hi), False, False)
-                    mm(pY(c), A("I%d" % (t + 1)), A("V", lo, hi), False, True)
+                    mm(pS(k), A("L%d" % (t + 1)), A("V", lo, hi), False, True)
+                    if z:
+                        mm(z, A("L%d" % (t + 1)), A("V", lo, hi), False, False)
+                    mm(pY(k), A(("J%d" if wide else "I%d") % (t + 1)), A("V", lo, hi), False, not wide)
             out.update({"A": scans(smax, lo, hi, True), "B": scans(smin, lo, hi, False, True),
                         "a": scans(smax, lo, mid, True), "b": scans(smin, lo, mid),
                         "x": scans(smax, mid, hi), "y": scans(smin, mid, hi, False, True), "d": d, "e": e})
+            if n == 4 * NC - 1:
+                out.update({"A": closing(True), "B": closing(False)})
             if t < 4:
-                out.update(tail(c, A("pB", 0, CW), lo, hi, lift))
+                out.update(tail(k, z, lo, hi, lift, wide, "s" if MOD == "S" and c in RS else "v"))
+                out["v"] = lambda: vgather(top, hi)
             return out
 
         chunks = {n: calls(n) for n in range(-NC, 4 * NC)}
-        for n in range(-NC, 4 * NC + 2):
-            for x in SLOT.split():
+        for n in range(-NC, 5 * NC):
+            for x in (LAST.get(4 * NC - n) or SLOT).split():
                 call = chunks.get(n - int(x[1]), {}).get(x[0])
                 if call:
                     call()
 
-    landed("ad", 3 * neng, [("RD", 12 * a + c) for a in peers for c in range(12)])
+    for a in peers:
+        landed("ad%d" % a, neng, A("RD", UN * a, UN * a + UN)[1])
     for bank in ("pA", "pB"):
         iota_row(bank)
     for n, a in enumerate([j] + peers):
@@ -552,14 +711,19 @@ def rank_program(g, core, T, topo):
             z = A("ZL" if a % 2 == 0 else "ZH", 96 - 32 * a, 224 - 32 * a)
             mm(A(bank, 0, UN), z, A("RD", UN * a, UN * a + UN), False, n == 3)
     sort("R1")
-    search(1, "R1", Xq, lift1, lambda: None)
-    tt(A("Xn"), ind(A("V"), A("R1")), Xq, ALU.add)
-    act(A("KM"), A("pA", 0, UN), ACT.Copy, acc=A("Acol", 0, 1))
-    act(A("Acol", 1, 2), A("Acol", 0, 1), ACT.Identity, bias=LC)
-    ts(A("Acol", 2, 3), A("Acol", 0, 1), LIFT - 2047.5, ALU.add)
-    lift2 = (A("Acol", 2, 3), A("Acol", 1, 2))
+    search(1, "R1", A("Xq"), lift1)
+    tt(A("Xn"), ind(A("V"), A("R1")), A("Xq"), ALU.add)
+    emit("v", lambda: g.vector.tensor_reduce(out=T.Acol[:, 2:3], in_=T.pB[:, :CW], axis=AxisListType.X, op=ALU.add),
+         [A("pB", 0, CW)], [A("Acol", 2, 3)])
+    ts(A("Acol", 3, 4), A("Acol", 2, 3), A("Acol", 1, 2), ALU.add)
+    ts(A("Acol", 4, 5), A("Acol", 2, 3), A("Acol", 1, 2), ALU.add, -2047.5, ALU.add)
+    act(A("Acol", 5, 6), A("Acol", 4, 5), ACT.Copy, scale=2.0 ** -12)
+    lift2 = (A("Acol", 4, 5), A("Acol", 3, 4), A("Acol", 5, 6))
 
-    columns(A("L"), A("I16"), "Xn", M2_S[0], lift2)
+    if WIDE == 4:
+        window[0] = 2 * W
+        window[1].extend(second)
+    columns(A("L"), A("EQ" if WIDE < 5 else "I16"), "Xn", CUT, lift2, WIDE < 5)
     for bank in ("pA", "pB"):
         iota_row(bank)
     done = [0]
@@ -570,13 +734,13 @@ def rank_program(g, core, T, topo):
             mm(A(bank, lo, hi), A("KWp"), last("mx", lo, hi), False, False)
             mm(A(bank, lo, hi), A("KWn"), last("mn", lo, hi), False, done[0] == UN)
 
-    measure(M2_S, M2_V, keys2)
+    measure(M2_S, M2_V, keys2, 1)
     mm(A("pY2", 0, UN), A("KWp"), last("mx", 0, UN), True, False)
     mm(A("pY2", 0, UN), A("KWn"), last("mn", 0, UN), False, True)
     sort("R2")
     act(A("qs"), A("pY2", 0, UN), ACT.Copy, scale=QS)
     fan(A("qs"), "lq", "aq")
-    search(2, "R2", A("Xn"), lift2, lambda: None)
+    search(2, "R2", A("Xn"), lift2)
 
     landed("aq", 3 * neng, [("lq", a) for a in peers])
     for a in [j] + peers:
@@ -585,8 +749,9 @@ def rank_program(g, core, T, topo):
         src = A(name, lo, lo + UN)
         dma("y", T.yq[2 * a:2 * a + 2, :], T[name][32 * j:32 * j + 32:16, lo:lo + UN], [src])
     tt(A("yo"), ind(A("V"), A("R2")), A("Xn"), ALU.add)
-    fan(A("yo"), "ly", "ay")
-    landed("ay", 3 * neng, [("ly", a) for a in peers])
+    fan(A("yo"), "ly", "ay%d" % j)
+    for a in peers:
+        landed("ay%d" % a, neng, [("ly", a)])
     for n, a in enumerate([j] + peers):
         lo = 0 if a == j else UN * a
         src = A("yo" if a == j else "ly", lo, lo + UN, None, 32 * j, 32 * j + 32)

from concourse.bass import DstId, RemoteDMATransfer
from concourse.mybir import AluOpType, AxisListType, ActivationFunctionType

ALU = AluOpType
ACT = ActivationFunctionType
UN = 192
NC = 3
CW = 64
GS = 32
LIFT = 160 * 4096.0
BAND = 1.5 * 2.0 ** 36
SLOT = "a0 f2 G3 d1 h2 e1 k2 b0 x0 r1 o0 y0 g2 q1"
COLUMNS = {False: "S0 r0 S1 Z1 m0 Y0 r1 q0 f0 Y1 q1 h0 k0 f1 g0 h1 k1",
           "r1": "K0 S0 S1 Y0 r0 m0 Z1 r1 q0 q1 f0 Y1 h0 k0 W0 g0 s0 t0 f1 h1 v0 k1 p0",
           "r2": "K0 S0 S1 W0 Y0 r0 s0 m0 Z1 r1 t0 q1 q0 f0 Y1 h0 k0 g0 f1 h1 v0 k1",
           True: "S0 S1 Z0 r0 Z1 Y0 r1 q0 f0 Y1 k0 q1 g0 f1 v0 k1"}
MOD, CMOD = "T", "VT"
SHARE = (0, 0, 0)
FIRST_V = 0
JOIN = 1
ZB = ("pB", "pB")
GL = 32
RS = (0, 1, 2)
VCOPY = "v"
LAST = {1: "G3 a0 d1 b0 e1 x0 y0"}
CUT = 64
M1_S, M1_V = (64, 48, 32, 16), 32
M2_S, M2_V = (32, 32, 48, 32, 16), 32
LAST_V = (0, 0, 0)
WIDE = 5
SORT_S = 7
EARLY = 64
AHEAD, LOADS = 2, 0
W = 8192
KEY = 2.0 ** 22
WHOLE = 1.5 * 2.0 ** 23

SCRATCH = {}
GRAN = {}


def _buf(names, cols, dtype, gran=None, where="sbuf"):
    for name in names.split():
        SCRATCH[name] = (where, [128, cols], dtype)
        GRAN[name] = gran if gran else cols


_buf("U32", UN, "int32")
_buf("Uq", UN, "int32")
_buf("shelfs", 2 * W, "bfloat16", 2048)
_buf("Xo Xq Xn Xs V ks kss yo qs w2", UN, "float32", 8)
_buf("ci cj", UN, "int32", 8)
_buf("off", UN, "uint16", 8)
_buf("gv mx mn", UN * 16, "bfloat16", 128)
_buf("B1 B2 B3 B4 rq rw sg tk stk", UN, "bfloat16", 8)
_buf("RD", 4 * UN, "bfloat16", 8)
_buf("lq ly", 4 * UN, "float32", UN)
_buf("KM Kc", UN, "float32")
_buf("cmp", 6 * UN, "bfloat16", UN)
_buf("cmps", 6 * UN, "bfloat16")
_buf("sj", 12 * UN, "bfloat16", UN)
_buf("acc", 16, "float32", 1)
_buf("R1 R2", 12, "uint16", 1)
_buf("Acol", 8, "float32", 1)
_buf("mmax mmin", 1024, "bfloat16")
_buf("rkm", 6 * UN, "bfloat16")
_buf("m16 diag uf uu", UN, "float32")
_buf("it big half neg", UN, "bfloat16")
_buf("ones", 96, "bfloat16")
_buf("nhalf RM RW", 128, "bfloat16")
_buf("mG mP1 mP2", 128, "float32")
_buf("ic", 24, "int32", 1)
_buf("fc", 96, "float32", 1)
_buf("SG TR L NEQ I16 EQ E16", 128, "float32")
for _r in "12":
    for _n in ("M0", "M1", "Y1", "DP", "SW", "PG"):
        _buf(_n + _r, 128, "float32")
    _buf("TWp%s TWn%s" % (_r, _r), 128, "bfloat16")
_buf("L2 L3 L4 I2 I3 I4 J2 J3 J4", 128, "float32")
_buf("AW1 AW2 AW3 AW4 CP1 CP2 CP3 CP4 KWp KWn", 128, "bfloat16")
_buf("ZL ZH", 224, "bfloat16")
_buf("pS0 pS1 pS2 pY0 pY1 pY2 pA pB", 512, "float32", None, "psum")
PSUM = {n for n in SCRATCH if SCRATCH[n][0] == "psum"}
SCRATCH["st"] = ("dram", [4, 128, 2048], "bfloat16")
SCRATCH["rv"] = ("dram", [4, 128, 2048], "bfloat16")
SCRATCH["su"] = ("dram", [4, 128, UN // 4], "int32")
SCRATCH["ru"] = ("dram", [4, 128, UN // 4], "int32")

NDMA = 28
SEMAPHORES = (["cv", "cs", "ct", "cg", "lo", "lr", "au", "aq"] + [n % a for n in ("as%d", "ad%d", "ay%d") for a in range(4)]
              + ["d%d" % k for k in range(NDMA)])


def rank_program(g, core, T, topo):
    rank = T.rank_of(core)
    if rank is None:
        return
    j = rank % 4
    quad = [T.cores[rank - j + a] for a in range(4)]
    peers = [j ^ 1, j ^ 2, j ^ 3]

    QUEUE = {"v": g.vector, "s": g.scalar, "t": g.tensor, "g": g, "y": g.sync}
    SEM = {"v": "cv", "s": "cs", "t": "ct", "g": "cg"}
    count = {}
    known = {q: {} for q in QUEUE}
    state = {}

    def need(q, tok):
        sem, n, who, clock = tok
        if known[q].get(sem, 0) >= n:
            return
        QUEUE[q].wait_ge(T.sem[sem], n)
        for s_, v_ in clock.items():
            if known[q].get(s_, 0) < v_:
                known[q][s_] = v_
        known[q][sem] = n

    def entry(k):
        return state.setdefault(k, {"w": None, "r": {}})

    def emit(q, call, reads=(), writes=(), dma=None):
        toks = []
        for ref in reads:
            for k in ref[1]:
                e = entry(k)
                if k[0] in PSUM:
                    toks += [t for t in e["r"].values() if t[2] != q]
                if e["w"] and not (k[0] in PSUM and q == "t"):
                    toks.append(e["w"])
        for ref in writes:
            for k in ref[1]:
                e = entry(k)
                if k[0] in PSUM:
                    toks += [t for t in e["r"].values() if t[2] != q or q != "t"]
                else:
                    if e["w"]:
                        toks.append(e["w"])
                    toks += list(e["r"].values())
        toks.sort(key=lambda t: -t[1])
        for t in toks:
            need(q, t)
        sem = dma if dma else SEM[q]
        inc = 16 if dma else 1
        call().then_inc(T.sem[sem], inc)
        count[sem] = count.get(sem, 0) + inc
        tok = (sem, count[sem], None if dma else q, dict(known[q]))
        for ref in reads:
            for k in ref[1]:
                state[k]["r"][sem] = tok
        for ref in writes:
            for k in ref[1]:
                if k[0] in PSUM:
                    state[k]["r"][sem] = tok
                    state[k]["w"] = None if q == "t" else tok
                else:
                    state[k] = {"w": tok, "r": {}}
        return tok

    def A(name, lo=0, hi=None, step=None, p0=0, p1=128):
        hi = SCRATCH[name][1][1] if hi is None else hi
        ap = T[name][p0:p1, lo:hi] if step is None else T[name][p0:p1, lo:hi:step]
        gr = GRAN[name]
        return (ap, [(name, k) for k in range(lo // gr, (hi - 1) // gr + 1)])

    def ind(win, off):
        return (win[0].indirect(off[0]), win[1] + off[1])

    def val(x):
        return x[0] if isinstance(x, tuple) else x

    def refs(*xs):
        return [x for x in xs if isinstance(x, tuple)]

    def tt(out, a, b, op):
        emit("v", lambda: g.vector.tensor_tensor(out=out[0], in0=a[0], in1=b[0], op=op), [a, b], [out])

    def ts(out, a, s1, op0, s2=None, op1=None):
        if op1 is None:
            emit("v", lambda: g.vector.tensor_scalar(out=out[0], in0=a[0], scalar1=val(s1), scalar2=None, op0=op0),
                 [a] + refs(s1), [out])
        else:
            emit("v", lambda: g.vector.tensor_scalar(out=out[0], in0=a[0], scalar1=val(s1), scalar2=val(s2), op0=op0, op1=op1),
                 [a] + refs(s1, s2), [out])

    def cp(out, a):
        emit("v", lambda: g.vector.tensor_copy(out=out[0], in_=a[0]), [a], [out])

    def scatter(win, off, a):
        emit("v", lambda: g.vector.tensor_copy(out=win[0].indirect(off[0]), in_=a[0]), [a, off], [win])

    def fill(out, x):
        emit("v", lambda: g.vector.memset(out[0], x), [], [out])

    def scan(out, a, b, init, op0, op1):
        emit("v", lambda: g.vector.tensor_tensor_scan(out=out[0], data0=a[0], data1=b[0], initial=init, op0=op0, op1=op1),
             [a, b], [out])

    def act(out, a, func, bias=None, scale=None, acc=None):
        kw = {}
        if bias is not None:
            kw["bias"] = val(bias)
        if scale is not None:
            kw["scale"] = val(scale)
        if acc is not None:
            kw["accum_out"] = acc[0]
        emit("s", lambda: g.scalar.activation(out=out[0], in_=a[0], func=func, **kw), [a] + refs(bias, scale), [out] + refs(acc))

    def mm(out, lhs, rhs, start=True, stop=True):
        emit("t", lambda: g.tensor.matmul(out=out[0], lhsT=lhs[0], rhs=rhs[0], start=start, stop=stop), [lhs, rhs], [out])

    def iota(ref, pattern, base=0, chan=0):
        if ref[1][0][0] == "ic":
            emit("g", lambda: g.iota(ref[0], pattern, base, chan), [], [ref])
        else:
            emit("g", lambda: g.iota(ref[0], pattern, base, chan, allow_small_or_imprecise_dtypes=True), [], [ref])

    def select(out, a, pattern, op, x, base=0, chan=0):
        emit("g", lambda: g.affine_select(out[0], a[0], pattern, op, x, base, chan), [a], [out])

    ndma = [0]

    def dma(q, out_ap, in_ap, reads=(), writes=()):
        sem = "d%d" % ndma[0]
        ndma[0] += 1
        return emit(q, lambda: QUEUE[q].dma_start(out_ap, in_ap), reads, writes, dma=sem)

    neng = len(topo.engines(core, quad[peers[0]]))

    def fan(src, dst_name, sem, left="lo"):
        for k in src[1]:
            need("g", state[k]["w"])
        ids = []
        for a in peers:
            rid, pid, _ = topo.addr(quad[a])
            ids.append(DstId(rid=rid, pnc=pid))
        dst = T[dst_name][:, UN * j:UN * j + UN]
        g.remote_dma_fused([RemoteDMATransfer(dst_ids=ids, dma_engine_mask=topo.mask(core, quad[peers[0]]),
                                              remote_sem=T.sem[sem], srcs=[src[0]], dsts=[dst, dst, dst])], local_sem=T.sem[left])
        count[left] = count.get(left, 0) + neng

    def landed(sem, n, keys):
        count[sem] = n
        for k in keys:
            state[k] = {"w": (sem, n, None, {}), "r": {}}

    def ic(k):
        return A("ic", k, k + 1)

    def fc(k):
        return A("fc", k, k + 1)

    def send(src, dst, sem, some):
        engines = topo.engines(core, quad[some[0]])
        part = 1 << ((len(engines) // len(some)).bit_length() - 1)
        transfers = []
        for n, a in enumerate(some):
            rid, pid, _ = topo.addr(quad[a])
            transfers.append(RemoteDMATransfer(dst_ids=[DstId(rid=rid, pnc=pid)], remote_sem=T.sem[sem], src=src[a], dst=dst[j],
                                               dma_engine_mask=sum(1 << e for e in engines[part * n:part * n + part])))
        g.remote_dma_fused(transfers, local_sem=T.sem.lo)
        count["lo"] = count.get("lo", 0) + part * len(some)
        return part

    staged = dma("s", T.su[:, :, :], T.units[:, :])
    dma("y", T.U32[:, :], T.units[:, :], [], [A("U32")])
    early = dma("y", T.shelfs[:EARLY, :W], T.shelf[:EARLY, :], [], [(None, [("early", 0)])])
    dma("y", T.shelfs[EARLY:, :W], T.shelf[EARLY:, :], [], [A("shelfs", 0, W)])
    window = [W, [early]]
    need("y", early)
    stage = {}
    for a in peers:
        stage[a] = dma("y", T.st[a], T.shelf[32 * a:32 * a + 32, :])

    iota(ic(0), [[0, 1]], 0, 1)
    iota(A("uu"), [[1, UN]])
    iota(A("uf"), [[0, 12], [1, 16]])
    iota(A("mG"), [[1, 8], [0, 16]])
    need("g", staged)
    came = send(T.su, T.ru, "au", peers)
    mm_, mi = A("uu", 0, 128), A("uf", 0, 128)
    fill(A("nhalf"), -1.0 / 256)
    ts(ic(1), ic(0), 15, ALU.bitwise_and)
    ts(ic(2), ic(0), 4, ALU.logical_shift_right)
    for k in range(7):
        ts(ic(3 + k), ic(0), k, ALU.logical_shift_right, 1, ALU.bitwise_and)
    fill(A("ones"), 1.0)
    cp(A("fc", 0, 10), A("ic", 0, 10))
    fill(A("big"), 2.0 ** 24)
    P_, PI, PG_ = fc(0), fc(1), fc(2)
    ts(A("NEQ"), mm_, P_, ALU.is_equal, -1.0, ALU.mult)

    def bits(base):
        return A("fc", base, base + 7)
    ts(bits(10), bits(3), -1.0, ALU.mult, 1.0, ALU.add)
    ts(bits(17), bits(3), -2.0, ALU.mult, 1.0, ALU.add)
    ts(bits(24), bits(3), 2.0, ALU.mult, -1.0, ALU.add)
    ts(bits(31), bits(3), 16.0, ALU.mult, -16.0, ALU.add)
    ts(bits(82), bits(3), 1.0, ALU.mult, -1.0, ALU.add)
    ts(bits(59), bits(3), -8192.0, ALU.mult, 4096.0, ALU.add)
    ts(fc(59), fc(3), -4096.0, ALU.mult, 2048.0, ALU.add)
    ts(A("TR"), mi, PI, ALU.is_ge)
    ts(A("SG"), A("mG"), PG_, ALU.is_equal)
    cp(A("Xo"), A("U32"))
    tt(A("L"), A("SG"), A("TR"), ALU.mult)
    ts(bits(38), bits(24), 448.0 + 2 * KEY, ALU.mult)
    ts(bits(45), bits(17), 512.0, ALU.mult)
    ts(bits(52), bits(24), 512.0, ALU.mult)
    LOWC, L16, L1, PB = ({t: fc(b + 4 - t) for t in (1, 2, 3, 4)} for b in (10, 31, 82, 59))
    SIDE, NS, THR = ({r: fc(b + 4 + r) for r in (1, 2)} for b in (17, 24, 38))
    K512, K512N = fc(52 + 6), fc(45 + 6)

    def scaled(out, a, col):
        act(A(out), A(a), ACT.Copy, scale=col)

    for name, x in (("I16", -16.0), ("RM", 4096.0), ("EQ", -1.0), ("E16", -1.0 / 16), ("RW", 8192.0))[:5 if WIDE < 5 else 2]:
        scaled(name, "NEQ", x)
    for t in (1, 2, 3, 4):
        scaled("CP%d" % t, "NEQ", PB[t])

    def pS(c, n=None):
        return A("pS%d" % c, 0, n or CW)

    def pT(c):
        return A("pS%d" % c, UN, UN + CW)

    def pY(c, n=None):
        return A("pY%d" % c, 0, n or CW)

    def tail(c, z, lo, hi, lift, wide, by="v"):
        y = pY(c, hi - lo)

        def r():
            if by == "s":
                act(A("rq", lo, hi), pS(c, hi - lo), ACT.Identity, bias=lift[2], scale=2.0 ** -12)
            else:
                ts(A("rq", lo, hi), pS(c, hi - lo), lift[0], ALU.add, 2.0 ** -12, ALU.mult)
            mm(z, A("RM"), A("rq", lo, hi), False, True)

        def q():
            act(A("w2", lo, hi), z, ACT.Square, bias=lift[1])
            if wide:
                mm(y, A("E16"), A("w2", lo, hi), False, False)

        def f():
            ts(A("rw", lo, hi), A("w2", lo, hi), 2.0 ** -17, ALU.mult, 128.5 - 2.0 ** -15, ALU.add)
            mm(y, A("RW"), A("rw", lo, hi), False, True)
        def square():
            tt(A("w2", lo, hi), A("cj", lo, hi), A("cj", lo, hi), ALU.mult)
            if wide:
                mm(y, A("E16"), A("w2", lo, hi), False, False)
        if z is None:
            out = {"r": lambda: ts(A("ci", lo, hi), pS(c, hi - lo), lift[1], ALU.add),
                   "m": lambda: ts(A("cj", lo, hi), A("ci", lo, hi), 4095, ALU.bitwise_and), "q": square}
        else:
            out = {"r": r, "q": q}
        if wide:
            out.update({"f": f, "k": lambda: ts(A("off", lo, hi), y, WHOLE + 129 * W, ALU.add, WHOLE, ALU.subtract)})
        else:
            out.update({"f": lambda: tt(A("ci", lo, hi), A("w2", lo, hi), y, ALU.add),
                        "h": lambda: ts(A("cj", lo, hi), A("ci", lo, hi), 4, ALU.arith_shift_right, W - 1, ALU.bitwise_and),
                        "k": lambda: cp(A("off", lo, hi), A("cj", lo, hi))})
        return out

    def opened(c, lo, hi, wide):
        mm(pY(c, hi - lo), A("nhalf"), A("half" if wide else "big", lo, hi), True, False)

    def columns(ls, ly, X, cut, lift, wide, suspects=None, order=None):
        parts = []
        for c, (lo, hi) in enumerate(((0, cut), (cut, UN))):
            if hi == lo:
                parts.append({})
                continue
            opened(c, lo, hi, wide)
            z = (pS, pY)[c](2, hi - lo) if CMOD[c] != "V" else None
            calls = tail(c, z, lo, hi, lift, wide, "s" if CMOD[c] == "S" else "v")
            calls["S"] = lambda c=c, lo=lo, hi=hi: mm(pS(c, hi - lo), ls, A(X, lo, hi))
            if z:
                calls["Z"] = lambda z=z, lo=lo, hi=hi: mm(z, ls, A(X, lo, hi), True, False)
            calls["Y"] = lambda c=c, lo=lo, hi=hi: mm(pY(c, hi - lo), ly, A(X, lo, hi), False, not wide)
            parts.append(calls)
        parts[0].update(suspects or {})
        if cut < UN:
            parts[0]["g"] = lambda: gather(0, GS)
        for x in (order or COLUMNS[wide]).split():
            call = parts[int(x[1])].get(x[0])
            if call:
                call()

    def ew(name, lo, hi):
        return A(name, 16 * lo, 16 * hi)

    def picks(q, lo, hi):
        for tok in window[1]:
            need(q, tok)
        return ind(A("shelfs", 0, window[0]), A("off", lo, hi))

    def gather(lo, hi):
        if hi > lo:
            act(ew("gv", lo, hi), picks("s", lo, hi), ACT.Copy)

    def vgather(lo, hi):
        if hi > lo:
            cp(ew("gv", lo, hi), picks("v", lo, hi))

    def smax(lo, hi):
        scan(ew("mx", lo, hi), A("mmax", 0, 16 * (hi - lo)), ew("gv", lo, hi), 0.0, ALU.min, ALU.max)

    def smin(lo, hi):
        scan(ew("mn", lo, hi), A("mmin", 0, 16 * (hi - lo)), ew("gv", lo, hi), 0.0, ALU.add, ALU.min)

    def last(name, lo, hi):
        return A(name, 16 * lo + 15, 16 * hi, 16)

    def measure(pieces, own, after, begun=0):
        cuts = [sum(pieces[:k]) for k in range(len(pieces) + 1)]
        for lo, hi in zip(cuts[begun:], cuts[begun + 1:]):
            gather(lo, hi)
        if begun and JOIN:
            del cuts[1]
        order = list(zip(cuts, cuts[1:]))
        if own:
            vgather(UN - own, UN)
            order = [(UN - own, UN)] + order
        for lo, hi in order:
            smax(lo, hi)
            smin(lo, hi)
            after(lo, hi)

    LC = fc(90)
    fill(LC, LIFT)
    fill(fc(95), (LIFT - 2047.5) / 4096)
    lift1 = (LIFT - 2047.5, LC, fc(95))
    fill(A("mmin"), 0.0)
    fill(fc(91), 512.0)
    fill(fc(92), -2.0)
    fill(A("mmin", 0, 1024, 16), 512.0)
    columns(A("L"), A("I16"), "Xo", UN, lift1, False)
    act(A("mmax"), A("mmin"), ACT.Identity, bias=fc(91), scale=-1.0)
    act(A("it"), A("uu"), ACT.Identity, bias=fc(92), scale=-2.0)
    Z0, Z15, Z15L, GB, QS = fc(66), fc(67), fc(68), fc(69), fc(70)
    ts(Z0, PI, 0.0, ALU.is_equal, -1.0, ALU.mult)
    ts(Z15, PI, 15.0, ALU.is_equal)
    ts(GB, PG_, float(-2 * j), ALU.add)
    ts(QS, NS[2], 1.0 / 512, ALU.mult)
    ts(Z15L, Z15, fc(10 + 5), ALU.mult, 8.0, ALU.mult)
    SRC, GRP, PAIR = {}, {}, {}
    for r, X in ((1, 32.0), (2, 64.0)):
        SRC[r], GRP[r], PAIR[r] = fc(71 + r), fc(74 + r), fc(77 + r)
        ts(fc(92 + r), SIDE[r], LOWC[1], ALU.mult)
        ts(PAIR[r], NS[r], X / 32, ALU.mult, PG_, ALU.subtract)
    for r, X in ((1, 32.0), (2, 64.0)):
        ts(SRC[r], fc(92 + r), X, ALU.mult, P_, ALU.add)
        ts(GRP[r], fc(92 + r), X / 16, ALU.mult, PG_, ALU.add)

    def pair_groups(r):
        ts(A("PG%d" % r), A("mP%d" % r), float(r), ALU.is_equal)
        ts(A("M0%d" % r), A("mG"), GRP[r], ALU.is_equal)

    def pair_sums(r):
        ts(A("Y1%d" % r), mm_, SRC[r], ALU.is_equal, 1.0 if r == 2 and WIDE < 5 else 16.0, ALU.mult)
        tt(A("M1%d" % r), A("M0%d" % r), A("TR"), ALU.mult)

    def pair_scaled(r):
        scaled("TWp%d" % r, "PG%d" % r, SIDE[r])
        scaled("TWn%d" % r, "PG%d" % r, NS[r])
        scaled("SW%d" % r, "PG%d" % r, Z0)

    fill(A("ZL"), 0.0)
    fill(A("neg"), -2 * KEY)
    ts(A("diag"), A("uf"), PI, ALU.is_equal)
    ts(A("ZL", 96, 128), A("mG", 0, 32), GB, ALU.is_equal, -512.0, ALU.mult)
    for r in (1, 2):
        act(A("mP%d" % r), A("mG"), ACT.Abs, bias=PAIR[r])

    share = {}

    def pass_on(some):
        for a in some:
            need("g", stage[a])
        part = send(T.st, T.rv, "as%d" % j, some)
        share.update({a: part for a in some})

    def ranges(lo, hi):
        tt(A("RD", UN * j + lo, UN * j + hi), last("mx", lo, hi), last("mn", lo, hi), ALU.subtract)

    todo = []

    def ranges_late(lo, hi):
        todo.append((lo, hi))
        if hi == UN - M1_V - M1_S[-1]:
            ranges(0, hi)
        if hi == UN - M1_V:
            ranges(lo, UN)

    for a in peers[:AHEAD]:
        pass_on([a])
    measure(M1_S, M1_V, ranges_late)
    fan(A("RD", UN * j, UN * j + UN), "RD", "ad%d" % j)
    g.sem_inc(T.sem.lr, 1)
    count["lr"] = 1
    if AHEAD < 3:
        pass_on(peers[AHEAD:])
    select(A("DP1"), A("NEQ"), [[-64, 2], [32, 2], [-1, 32]], ALU.not_equal, 1.0, -32, 1)
    select(A("DP2"), A("NEQ"), [[64, 2], [-1, 64]], ALU.not_equal, 1.0, -64, 1)

    act(A("ZH"), A("ZL"), ACT.Copy, scale=-1.0)
    fill(A("rkm", 0, (12 - SORT_S) * UN), 256.0)
    ts(A("m16"), A("uf"), 0.0, ALU.is_gt)
    LARGER = fc(89)
    fill(LARGER, 2 * KEY - 63)
    fill(A("rkm", 0, (12 - SORT_S) * UN, UN), 0.0)
    pair_groups(1)
    pair_sums(1)
    if WIDE < 5:
        fill(A("half"), 0.5)
    for t in (2, 3, 4):
        scaled("L%d" % t, "L", LOWC[t])
        if WIDE < 5:
            scaled("J%d" % t, "NEQ", L1[t])
    for t in range(2, min(WIDE, 4) + 1):
        scaled("I%d" % t, "NEQ", L16[t])
    pair_scaled(1)
    scaled("AW1", "PG1", Z15L)
    scaled("AW4", "PG1", Z15)
    for t in (2, 3):
        act(A("AW%d" % t), A("AW1"), ACT.Copy, scale=2.0 ** (1 - t))

    landed("au", 3 * came, [("ru", 0)])
    dma("y", T.Uq[32 * j:32 * j + 32, :], T.units[32 * j:32 * j + 32, :], [], [(None, [("Uq4", j)])])
    for a in peers:
        dma("y", T.Uq[32 * a:32 * a + 32, :], T.ru[a], [(None, [("ru", 0)])], [(None, [("Uq4", a)])])
    own_reads = list(state[("shelfs", 0)]["r"].values())
    for n, a in enumerate(peers):
        if n == LOADS:
            need("y", ("lr", 1, None, {}))
        landed("as%d" % a, share[a], [("rv", a)])
        for t in own_reads:
            need("y", t)
        window[1].append(dma("y", T.shelfs[32 * a:32 * a + 32, :W], T.rv[a], [(None, [("rv", a)])], []))
    second = []
    if WIDE < 5:
        second.append(dma("y", T.shelfs[32 * j:32 * j + 32, W:], T.shelf[32 * j:32 * j + 32, :]))
        for a in peers:
            second.append(dma("y", T.shelfs[32 * a:32 * a + 32, W:], T.rv[a], [(None, [("rv", a)])], []))

    def iota_row(bank):
        mm(A(bank, 0, UN), A("nhalf"), A("neg"), True, False)
        mm(A(bank, 0, UN), A("nhalf"), A("it"), False, False)

    def sort(R):
        nv = 12 - SORT_S
        tt(A("KM"), A("pA", 0, UN), A("diag"), ALU.mult)
        act(A("ks"), A("pB", 0, UN), ACT.Copy)
        scan(A("Kc"), A("m16"), A("KM"), 0.0, ALU.mult, ALU.add)

        def key(k):
            return A("Kc", 16 * k + 15, 16 * k + 16)
        for k in range(SORT_S):
            act(A("sj", UN * k, UN * k + UN), A("ks"), ACT.Sign, bias=key(k), scale=-1.0, acc=A("acc", k, k + 1))
        for k in range(nv):
            ts(A("cmp", UN * k, UN * k + UN), A("ks"), key(SORT_S + k), ALU.is_lt)
        if R == "R1":
            cp(A("Xq"), (T.Uq[:, :], [("Uq4", a) for a in range(4)]))
        scan(A("cmps", 0, nv * UN), A("rkm", 0, nv * UN), A("cmp", 0, nv * UN), 0.0, ALU.min, ALU.add)
        cp(A(R, SORT_S, 12), A("cmps", UN - 1, nv * UN, UN))
        ts(A(R, 0, SORT_S), A("acc", 0, SORT_S), 0.5, ALU.mult, 95.5, ALU.add)

    def search(r, R, X, lift):
        TWp, TWn = A("TWp%d" % r), A("TWn%d" % r)
        scatter(A("Xs"), A(R), X)
        if r == 1:
            pair_groups(2)
            late = lambda: pair_sums(2)
        else:
            late = None

        def suspects():
            mm(A("pA", 0, UN), A("DP%d" % r), A("Xs"))
            if VCOPY == "s":
                act(A("V"), A("pA", 0, UN), ACT.Copy)
            else:
                cp(A("V"), A("pA", 0, UN))
        far = A("pB", 0, UN)
        more = {"v": suspects, "p": late, "u": lambda: vgather(UN - FIRST_V, UN),
                "K": lambda: emit("s", lambda: g.scalar.activation(out=T.kss[:, :].indirect(A(R)[0]), in_=T.ks[:, :], func=ACT.Silu),
                                  [A("ks"), A(R)], [A("kss")]),
                "W": lambda: mm(far, A("SW%d" % r), A("kss")),
                "s": lambda: act(A("sg"), far, ACT.Sign, bias=LARGER),
                "t": lambda: act(A("tk"), far, ACT.Sign, bias=THR[r], scale=NS[r])}
        columns(A("M1%d" % r), A("Y1%d" % r), "Xs", CUT, lift, r == 2 and WIDE < 5, more, COLUMNS.get("r%d" % r))
        after_max = {2 * NC: lambda: tt(A("stk"), A("sg"), A("tk"), ALU.mult)}

        def calls(n):
            t, c = n // NC + 1, n % NC
            lo, mid, hi = CW * c, CW * c + GS, CW * c + CW
            gmid = lo + GL if n == 3 * NC - 1 else mid
            if n == 4 * NC - 1:
                mid = lo + GL
            wide = (r == 2 and WIDE < 5) or t >= WIDE
            top = hi - (LAST_V[c] if t == 3 else SHARE[c] if t > 0 else FIRST_V if c == NC - 1 else 0)
            out = {}

            def first_part():
                if r == 1 and t == WIDE and c == 0:
                    window[0] = 2 * W
                    window[1].extend(second)
                if n > -NC:
                    gather(lo, gmid)
            if t < 4:
                out["g"] = first_part
                out["G"] = lambda: gather(gmid, top)
            if t < 1:
                return out
            k = n % 3
            z = A(ZB[n % 2], 0, CW) if MOD != "V" else None
            bt = A("B%d" % t, lo, hi) if r == 1 else A("pY%d" % k, UN, UN + CW)

            def sides():
                for s in ("sg", "stk")[:1 + t // 4]:
                    mm(pT(k), A("CP%d" % t), A(s, lo, hi), False, False)

            def opening():
                mm(pT(k), A("nhalf"), A("ones", 0, CW), True, False)
                sides()

            def own():
                if t < 4:
                    opened(k, lo, hi, wide)
                    mm(pY(k), A("EQ" if wide else "I16"), A("Xs", lo, hi), False, False)
            out["o"] = own

            def scans(f, a, b, first=False, end=False):
                def call():
                    if first:
                        opening()
                    f(a, b)
                    if first and n in after_max:
                        after_max[n]()
                    if b == hi:
                        mm(pT(k), TWp if f is smax else TWn, last("mx" if f is smax else "mn", lo, hi), False, end)
                return call

            def closing(first):
                cut = hi - LAST_V[c]

                def call():
                    if first:
                        opening()
                    for a, b in ((lo, mid), (cut, hi)) if first else ((mid, cut),):
                        if b > a:
                            smax(a, b)
                            smin(a, b)
                    if not first:
                        mm(pT(k), TWp, last("mx", lo, hi), False, False)
                        mm(pT(k), TWn, last("mn", lo, hi), False, True)
                return call

            def d():
                if r == 1 and n == 4 * NC - 1:
                    pair_scaled(2)
                    scaled("KWp", "SG", K512)
                    scaled("KWn", "SG", K512N)
                ts(bt, pT(k), BAND, ALU.add, BAND, ALU.not_equal)
                if t < 4:
                    mm(pS(k), A("L"), A("Xs", lo, hi), True, False)
                    if z:
                        mm(z, A("L"), A("Xs", lo, hi), True, False)
                if r == 1 and t == 4 and c < NC - 1:
                    mm(A("pA", lo, hi), A("AW4"), bt, False, c == NC - 2)
                    if c == NC - 2:
                        act(A("KM", 0, hi), A("pA", 0, hi), ACT.Copy, acc=A("Acol", 0, 1))
                        act(A("Acol", 1, 2), A("Acol", 0, 1), ACT.Identity, bias=LC)
                if r == 1 and t < 4 and c == NC - 2:
                    mm(A("pA", 0, hi), A("AW%d" % t), A("B%d" % t, 0, hi), t == 1, False)
                if r == 1 and n == 4 * NC - 2:
                    for s in (1, 2, 3):
                        mm(A("pB", 0, CW), A("AW%d" % s), A("B%d" % s, hi, UN), s == 1, False)
                if r == 1 and n == 4 * NC - 1:
                    mm(A("pB", 0, CW), A("AW4"), bt, False, True)

            def e():
                tt(A("V", lo, hi), bt, A("V", lo, hi), ALU.mult)
                if t < 4:
                    mm(pS(k), A("L%d" % (t + 1)), A("V", lo, hi), False, True)
                    if z:
                        mm(z, A("L%d" % (t + 1)), A("V", lo, hi), False, False)
                    mm(pY(k), A(("J%d" if wide else "I%d") % (t + 1)), A("V", lo, hi), False, not wide)
            out.update({"A": scans(smax, lo, hi, True), "B": scans(smin, lo, hi, False, True),
                        "a": scans(smax, lo, mid, True), "b": scans(smin, lo, mid),
                        "x": scans(smax, mid, hi), "y": scans(smin, mid, hi, False, True), "d": d, "e": e})
            if n == 4 * NC - 1:
                out.update({"A": closing(True), "B": closing(False)})
            if t < 4:
                out.update(tail(k, z, lo, hi, lift, wide, "s" if MOD == "S" and c in RS else "v"))
                out["v"] = lambda: vgather(top, hi)
            return out

        chunks = {n: calls(n) for n in range(-NC, 4 * NC)}
        for n in range(-NC, 5 * NC):
            for x in (LAST.get(4 * NC - n) or SLOT).split():
                call = chunks.get(n - int(x[1]), {}).get(x[0])
                if call:
                    call()

    for a in peers:
        landed("ad%d" % a, neng, A("RD", UN * a, UN * a + UN)[1])
    for bank in ("pA", "pB"):
        iota_row(bank)
    for n, a in enumerate([j] + peers):
        for bank in ("pA", "pB"):
            z = A("ZL" if a % 2 == 0 else "ZH", 96 - 32 * a, 224 - 32 * a)
            mm(A(bank, 0, UN), z, A("RD", UN * a, UN * a + UN), False, n == 3)
    sort("R1")
    search(1, "R1", A("Xq"), lift1)
    tt(A("Xn"), ind(A("V"), A("R1")), A("Xq"), ALU.add)
    emit("v", lambda: g.vector.tensor_reduce(out=T.Acol[:, 2:3], in_=T.pB[:, :CW], axis=AxisListType.X, op=ALU.add),
         [A("pB", 0, CW)], [A("Acol", 2, 3)])
    ts(A("Acol", 3, 4), A("Acol", 2, 3), A("Acol", 1, 2), ALU.add)
    ts(A("Acol", 4, 5), A("Acol", 2, 3), A("Acol", 1, 2), ALU.add, -2047.5, ALU.add)
    act(A("Acol", 5, 6), A("Acol", 4, 5), ACT.Copy, scale=2.0 ** -12)
    lift2 = (A("Acol", 4, 5), A("Acol", 3, 4), A("Acol", 5, 6))

    if WIDE == 4:
        window[0] = 2 * W
        window[1].extend(second)
    columns(A("L"), A("EQ" if WIDE < 5 else "I16"), "Xn", CUT, lift2, WIDE < 5)
    for bank in ("pA", "pB"):
        iota_row(bank)
    done = [0]

    def keys2(lo, hi):
        done[0] += hi - lo
        for bank in ("pA", "pB"):
            mm(A(bank, lo, hi), A("KWp"), last("mx", lo, hi), False, False)
            mm(A(bank, lo, hi), A("KWn"), last("mn", lo, hi), False, done[0] == UN)

    measure(M2_S, M2_V, keys2, 1)
    mm(A("pY2", 0, UN), A("KWp"), last("mx", 0, UN), True, False)
    mm(A("pY2", 0, UN), A("KWn"), last("mn", 0, UN), False, True)
    sort("R2")
    act(A("qs"), A("pY2", 0, UN), ACT.Copy, scale=QS)
    fan(A("qs"), "lq", "aq")
    search(2, "R2", A("Xn"), lift2)

    landed("aq", 3 * neng, [("lq", a) for a in peers])
    for a in [j] + peers:
        lo = 0 if a == j else UN * a
        name = "qs" if a == j else "lq"
        src = A(name, lo, lo + UN)
        dma("y", T.yq[2 * a:2 * a + 2, :], T[name][32 * j:32 * j + 32:16, lo:lo + UN], [src])
    tt(A("yo"), ind(A("V"), A("R2")), A("Xn"), ALU.add)
    fan(A("yo"), "ly", "ay%d" % j)
    for a in peers:
        landed("ay%d" % a, neng, [("ly", a)])
    for n, a in enumerate([j] + peers):
        lo = 0 if a == j else UN * a
        src = A("yo" if a == j else "ly", lo, lo + UN, None, 32 * j, 32 * j + 32)
        dma("s" if n % 2 else "y", T.yu[32 * a:32 * a + 32, :], src[0], [src])
    for sem, n in sorted(count.items()):
        if known["y"].get(sem, 0) < n:
            g.sync.wait_ge(T.sem[sem], n)
